import numpy as np
import ml_dtypes


def mxq(x, axis, fmt="e4m3"):
    dtype, down = {"e4m3": (ml_dtypes.float8_e4m3fn, 7), "e5m2": (ml_dtypes.float8_e5m2, 14)}[fmt]
    v = np.moveaxis(np.asarray(x, np.float32).astype(ml_dtypes.bfloat16).astype(np.float64), axis, -1)
    blocks = v.reshape(v.shape[:-1] + (-1, 32))
    amax = np.abs(blocks).max(-1, keepdims=True)
    byte = np.maximum(np.where(amax > 0, np.frexp(amax)[1] - 1 + 127, 0) - down, 1)
    scale = np.exp2(byte - 127.0)
    codes = (blocks / scale).astype(np.float32).astype(dtype).astype(np.float64)
    return np.moveaxis((codes * scale).reshape(v.shape), -1, axis)


WIDE = False


def mx_kscale(k):
    if not WIDE:
        return np.ones(k)
    levels = np.array([10, -10, 5, -5, 0])
    if k % 512:
        return np.exp2(np.random.permutation(np.resize(levels, k // 32))).repeat(32)
    a = np.empty((k // 512, 16))
    for p in range(k // 512):
        a[p, :8] = np.random.permutation(np.resize(levels, 8))
        for g in range(8):
            far = levels[np.abs(levels - a[p, g]) >= 10]
            a[p, g + 8] = far[np.random.randint(len(far))]
    return np.exp2(a.ravel()).repeat(32)


def f64(x):
    return np.asarray(x).astype(np.float64)


def striped(idx):
    return np.tile(idx.reshape(-1, 16).T, (8, 1)).astype(np.uint16)


def unstriped(offs):
    return offs[:16].T.reshape(-1).astype(np.int64)


E2M1 = np.array([0.0, 0.5, 1.0, 1.5, 2.0, 3.0, 4.0, 6.0, -0.0, -0.5, -1.0, -1.5, -2.0, -3.0, -4.0, -6.0])


def pack_weight(w, fmt):
    k, n = w.shape
    w = f64(np.asarray(w, np.float32).astype(ml_dtypes.bfloat16)).reshape(k // 32, 32, n)
    amax = np.abs(w).max(1)
    if fmt == "e4m3":
        byte = np.frexp(amax)[1] - 1 + 127 - 7
    else:
        mant, ex = np.frexp(amax / 6.0)
        byte = np.where(mant > 0.5, ex, ex - 1) + 127
    byte = np.clip(np.where(amax > 0, byte, 1), 1, 254)
    scaled = (w * np.exp2(127.0 - byte)[:, None, :]).reshape(k, n).astype(np.float32)
    by_word = np.ascontiguousarray(scaled.reshape(k // 512, 128, 4, n).transpose(0, 1, 3, 2))
    if fmt == "e4m3":
        words = by_word.astype(ml_dtypes.float8_e4m3fn).view(np.uint8)
    else:
        c = by_word.astype(ml_dtypes.float4_e2m1fn).view(np.uint8) & 0xF
        words = (c[..., 0::2] | (c[..., 1::2] << 4)).reshape(k // 512, 128, 2 * n)
    return np.ascontiguousarray(words), np.ascontiguousarray(byte.astype(np.uint8).reshape(k // 512, 16, n))


def unpack_weight(words, scales, fmt):
    g, _, n = scales.shape
    words = np.ascontiguousarray(words).reshape(g, 128, n, -1)
    if fmt == "e4m3":
        vals = words.view(ml_dtypes.float8_e4m3fn).astype(np.float64)
    else:
        nib = np.empty((g, 128, n, 4), np.uint8)
        nib[..., 0::2] = words & 0xF
        nib[..., 1::2] = words >> 4
        vals = E2M1[nib]
    vals = vals * np.repeat(np.exp2(scales.astype(np.float64) - 127.0), 8, axis=1)[..., None]
    return vals.transpose(0, 1, 3, 2).reshape(g * 512, n)


def relu2(v):
    return np.maximum(v, 0.0) ** 2


K, T, E, C, N = 1536, 512, 8, 256, 128
TOP = 4


def by_expert(wq, xq):
    return np.concatenate([wq[e].T @ xq[:, e * C:(e + 1) * C] for e in range(E)], axis=1)


def setup_inputs():
    n = np.random.standard_normal
    s = mx_kscale(K)[:, None]
    deal = np.repeat(np.arange(E), C).reshape(TOP, T)[:, np.random.permutation(T)]
    deal = np.take_along_axis(deal, np.argsort(np.random.rand(TOP, T), axis=0), axis=0)
    for _ in range(8):
        s_, t_ = np.random.permutation(T).reshape(2, -1); r = np.random.randint(TOP, size=T // 2); x, y = deal[r, s_].copy(), deal[r, t_].copy()
        ok = ~((deal[:, s_] == y).any(0) | (deal[:, t_] == x).any(0)); deal[r[ok], s_[ok]] = y[ok]; deal[r[ok], t_[ok]] = x[ok]
    order = np.lexsort((np.random.rand(TOP * T), deal.reshape(-1)))
    slot_token = order % T; pos = np.empty(TOP * T, np.int64); pos[order] = np.arange(TOP * T); pos = pos.reshape(TOP, T)
    g = np.random.uniform(0.5, 1.5, (TOP, T)); g = g / g.sum(0)
    w = [pack_weight(m, "e2m1") for m in n((E, K, N)) / np.sqrt(K) / s[None]]
    return {
        "xT": (n((K, T)) * s).astype(np.float32),
        "w_words": np.stack([m[0] for m in w]),
        "w_scales": np.stack([m[1] for m in w]),
        "b": (0.3 * n((N, E))).astype(np.float32),
        "gate": np.stack([np.tile(r, (N, 1)) for r in g]).astype(np.float32),
        "offs": striped(slot_token),
        "pos1": striped(pos[0]),
        "pos2": striped(pos[1]),
        "pos3": striped(pos[2]),
        "pos4": striped(pos[3]),
    }


def reference(xT, w_words, w_scales, b, gate, offs, pos1, pos2, pos3, pos4):
    idx = unstriped(offs)
    w = np.stack([unpack_weight(w_words[e], w_scales[e], "e2m1") for e in range(E)])
    xq = mxq(f64(xT)[:, idx], 0, "e4m3")
    y = by_expert(w, xq)
    y = relu2(y + np.repeat(f64(b), C, axis=1))
    return sum(f64(gate[r]) * y[:, unstriped(p)] for r, p in enumerate((pos1, pos2, pos3, pos4)))

@@ -1,0 +1,219 @@
+from contextlib import ExitStack
+
+import concourse.mybir as mybir
+
+K, T, E, C, N = 1536, 512, 8, 256, 128
+TOP = 4
+SLOTS = E * C
+P = 128
+A = K // 512
+FLOPS = 2 * K * N * SLOTS
+
+F32 = mybir.dt.float32
+BF16 = mybir.dt.bfloat16
+I32 = mybir.dt.int32
+U32 = mybir.dt.uint32
+U16 = mybir.dt.uint16
+U8 = mybir.dt.uint8
+FP8X4 = mybir.dt.float8_e4m3fn_x4
+FP4X4 = mybir.dt.float4_e2m1fn_x4
+ACT = mybir.ActivationFunctionType
+ALU = mybir.AluOpType
+
+
+def tile_moe_tk_lin_relu2_kernel(
+    tc, xT, w_words, w_scales, b, gate, offs, pos1, pos2, pos3, pos4, out
+):
+    nc = tc.nc
+    with ExitStack() as ctx:
+        keep = ctx.enter_context(tc.tile_pool(name="keep", bufs=1))
+        ring = ctx.enter_context(tc.tile_pool(name="ring", bufs=3))
+        psum = ctx.enter_context(tc.psum_pool(name="psum", bufs=8))
+
+        offs_t = keep.tile([P, SLOTS // 16], U16, name="offs_t")
+        pos_t = [keep.tile([P, T // 16], U16, name=f"pos_t{r}") for r in range(TOP)]
+        x_raw = [keep.tile([P, 4, T], F32, name=f"x_raw{a}") for a in range(A)]
+        x_bf = [keep.tile([P, T, 4], BF16, name=f"x_bf{a}", tag=f"share{a}", align_bytes=64) for a in range(A)]
+        span = [1376, 1376, 704]
+        codes = [keep.tile([P, span[a]], I32, name=f"codes{a}", align_bytes=64) for a in range(A)]
+        planes = keep.tile([P, 1376], U8, name="planes", align_bytes=64)
+        slot_codes = [[None, None], [None, None], [None, None]]
+        slot_planes = [keep.tile([P, SLOTS], U8, name=f"slot_planes{a}", align_bytes=64) for a in range(A)]
+        w_t = keep.tile([P, E * A, 2 * N], U8, name="w_t", align_bytes=64)
+        ws_t = keep.tile([P, E * A, N], U8, name="ws_t", align_bytes=64)
+        b_t = keep.tile([P, E], F32, name="b_t")
+        gate_t = keep.tile([P, TOP, T], F32, name="gate_t")
+        y_t = keep.tile([P, SLOTS], F32, name="y_t")
+        prod = [keep.tile([P, T], F32, name=f"prod{r}") for r in range(TOP)]
+        sums = [keep.tile([P, T], F32, name=f"sums{r}") for r in range(3)]
+        warm = keep.tile([P, 2], F32, name="warm")
+
+        def x_rows(a):
+            return xT[a * 512 : (a + 1) * 512, :].rearrange("(p j) t -> p j t", j=4)
+
+        half = T // 2
+        nc.sync.dma_start(out=x_raw[0][:, :, 0:half], in_=x_rows(0)[:, :, 0:half])
+        nc.sync.dma_start(out=x_raw[0][:, :, half:T], in_=x_rows(0)[:, :, half:T])
+        nc.sync.dma_start(offs_t[:], offs)
+        nc.sync.dma_start(out=x_raw[1][:], in_=x_rows(1))
+        nc.sync.dma_start(out=x_raw[2][:], in_=x_rows(2))
+
+        w_rows = w_words.rearrange("e a p c -> p (e a) c")
+        ws_rows = w_scales.rearrange("e a q n -> q (e a) n")
+        nc.gpsimd.memset(ws_t[:].rearrange("p i n -> p (i n)").bitcast(I32), 0)
+        nc.sync.dma_start(out=w_t[:].bitcast(I32), in_=w_rows.bitcast(I32))
+        for q in range(4):
+            nc.sync.dma_start(
+                out=ws_t[32 * q : 32 * q + 4, :, :].bitcast(I32),
+                in_=ws_rows[4 * q : 4 * q + 4, :, :].bitcast(I32),
+            )
+        nc.sync.dma_start(out=b_t[:], in_=b)
+        for r, pos in enumerate((pos1, pos2, pos3, pos4)):
+            nc.sync.dma_start(pos_t[r][:], pos)
+        nc.sync.dma_start(out=gate_t[:], in_=gate.rearrange("r p t -> p r t"))
+
+        nc.vector.memset(warm[:, 0:1], 0.0)
+        nc.scalar.activation(warm[:, 1:2], warm[:, 0:1], ACT.Relu)
+        nc.vector.memset(planes[:].bitcast(I32), 0)
+        for a in range(A):
+            nc.vector.memset(codes[a][:, T:], 0)
+        for a in (1, 2):
+            nc.gpsimd.memset(slot_planes[a][:].bitcast(I32), 0)
+
+        def interleave(copy, a, t0, t1):
+            copy(x_bf[a][:, t0:t1, :], x_raw[a][:, :, t0:t1].rearrange("p j t -> p t j"))
+
+        def quantise(a, t0, t1):
+            nc.vector.quantize_mx(
+                out=codes[a][:, t0:t1].bitcast(FP8X4),
+                scales=planes[4 * a : P, t0:t1],
+                in_=x_bf[a][:, t0:t1, :].rearrange("p t j -> p (t j)"),
+            )
+
+        def gather_words(a, s0, s1):
+            i = s0 // 1024
+            if slot_codes[a][i] is None:
+                tag = "share2" if (a, i) == (1, 1) else f"slot_codes{a}_{i}"
+                slot_codes[a][i] = keep.tile([P, 1024], I32, name=f"slot_codes{a}_{i}", tag=tag, align_bytes=64)
+            nc.vector.tensor_copy(
+                slot_codes[a][i][:, s0 - 1024 * i : s1 - 1024 * i].bitcast(U32),
+                codes[a][:].bitcast(U32).indirect(offs_t[:, s0 // 16 : s1 // 16]),
+            )
+
+        def gather_bytes(s0, s1):
+            nc.vector.tensor_copy(slot_planes[0][:, s0:s1], planes[:].indirect(offs_t[:, s0 // 16 : s1 // 16]))
+            for a in (1, 2):
+                for q in range(4):
+                    nc.sync.dma_start(
+                        out=slot_planes[a][32 * q : 32 * q + 4, s0:s1].bitcast(I32),
+                        in_=slot_planes[0][32 * q + 4 * a : 32 * q + 4 * a + 4, s0:s1].bitcast(I32),
+                    )
+
+        acc = {}
+
+        def multiply(e, h, passes):
+            cols = slice(e * C + h * N, e * C + h * N + N)
+            for a in passes:
+                nc.tensor.matmul_mx(
+                    out=acc[(e, h)],
+                    lhsT=w_t[:, e * A + a, :].bitcast(FP4X4),
+                    lhsT_scale=ws_t[:, e * A + a, :],
+                    rhs=slot_codes[a][e // 4][:, (e % 4) * C + h * N : (e % 4) * C + h * N + N].bitcast(FP8X4),
+                    rhs_scale=slot_planes[a][:, cols],
+                    start=(a == 0),
+                    stop=(a == A - 1),
+                )
+
+        def open_bank(e):
+            bank = psum.tile([P, 512], F32, name="acc")
+            for h in range(2):
+                acc[(e, h)] = bank[:, h * N : (h + 1) * N]
+            acc[e] = bank
+
+        def finish(es):
+            rels = {}
+            for e in es:
+                rels[e] = ring.tile([P, C], F32, name="rel")
+                nc.scalar.activation(rels[e][:], acc[e][:, 0:C], ACT.Relu, bias=b_t[:, e : e + 1])
+            for e in es:
+                nc.scalar.activation(y_t[:, e * C : (e + 1) * C], rels[e][:], ACT.Square)
+
+        interleave(nc.vector.tensor_copy, 0, 0, 256)
+        quantise(0, 0, 256)
+        interleave(nc.scalar.copy, 0, 432, 512)
+        interleave(nc.vector.tensor_copy, 0, 256, 432)
+        quantise(0, 256, 512)
+        gather_words(0, 0, 1024)
+        interleave(nc.scalar.copy, 1, 0, 512)
+        gather_words(0, 1024, 2048)
+        quantise(1, 0, 512)
+        interleave(nc.scalar.copy, 2, 0, 512)
+        gather_words(1, 0, 1024)
+        quantise(2, 0, 512)
+        gather_bytes(0, 1024)
+        gather_bytes(1024, 2048)
+        for e in range(4):
+            open_bank(e)
+            multiply(e, 0, (0,))
+        for e in range(4):
+            multiply(e, 0, (1,))
+        rel_pair = [keep.tile([P, 2 * C], F32, name=f"rel_pair{i}") for i in range(2)]
+        for i in range(2):
+            gather_words(2, 512 * i, 512 * i + 512)
+            for e in (2 * i, 2 * i + 1):
+                multiply(e, 0, (2,))
+                multiply(e, 1, (0, 1, 2))
+        for e in range(4):
+            nc.scalar.activation(
+                rel_pair[e // 2][:, (e % 2) * C : (e % 2 + 1) * C], acc[e][:, 0:C], ACT.Relu, bias=b_t[:, e : e + 1]
+            )
+            if e >= 2:
+                i = e - 2
+                nc.scalar.activation(y_t[:, 512 * i : 512 * i + 512], rel_pair[i][:], ACT.Square)
+        gather_words(1, 1024, 1536)
+        for e in (4, 5):
+            open_bank(e)
+            multiply(e, 0, (0, 1))
+        gather_words(2, 1024, 1536)
+        for e in (4, 5):
+            multiply(e, 0, (2,))
+            multiply(e, 1, (0, 1, 2))
+        finish((4, 5))
+        gather_words(1, 1536, 2048)
+        open_bank(6)
+        multiply(6, 0, (0, 1))
+        for h in range(2):
+            acc[(7, h)] = psum.tile([P, 512], F32, name="acc")[:, 0:N]
+            multiply(7, h, (0, 1))
+        gather_words(2, 1536, 1792)
+        multiply(6, 0, (2,))
+        multiply(6, 1, (0, 1, 2))
+        finish((6,))
+        gather_words(2, 1792, 2048)
+        for h in range(2):
+            multiply(7, h, (2,))
+        rel7 = [keep.tile([P, N], F32, name=f"rel7_{h}") for h in range(2)]
+        for h in range(2):
+            nc.vector.tensor_scalar(rel7[h][:], acc[(7, h)], b_t[:, 7:8], 0.0, ALU.add, ALU.max)
+        for h in range(2):
+            nc.vector.tensor_tensor(y_t[:, 7 * C + h * N : 7 * C + (h + 1) * N], rel7[h][:], rel7[h][:], ALU.mult)
+
+        def fetch(r, t0, t1):
+            nc.vector.tensor_tensor(
+                prod[r][:, t0:t1],
+                y_t[:].indirect(pos_t[r][:, t0 // 16 : t1 // 16]),
+                gate_t[:, r, t0:t1],
+                ALU.mult,
+            )
+
+        fetch(0, 0, T)
+        fetch(1, 0, T)
+        fetch(2, 0, T)
+        nc.vector.tensor_tensor(sums[0][:], prod[0][:], prod[1][:], ALU.add)
+        fetch(3, 0, T)
+        halves = (slice(0, half), slice(half, T))
+        for cols in halves:
+            nc.vector.tensor_tensor(sums[1][:, cols], sums[0][:, cols], prod[2][:, cols], ALU.add)
+        for cols in halves:
+            nc.vector.tensor_tensor(sums[2][:, cols], sums[1][:, cols], prod[3][:, cols], ALU.add)
+            nc.sync.dma_start(out=out[:, cols], in_=sums[2][:, cols])

@@ -1,6 +1,7 @@
 from contextlib import ExitStack
 
 import concourse.mybir as mybir
+from concourse.masks import make_identity
 
 K, T, E, C, N = 1536, 512, 8, 256, 128
 TOP = 4
@@ -32,7 +33,10 @@ def tile_moe_tk_lin_relu2_kernel(
 
         offs_t = keep.tile([P, SLOTS // 16], U16, name="offs_t")
         pos_t = [keep.tile([P, T // 16], U16, name=f"pos_t{r}") for r in range(TOP)]
-        x_raw = [keep.tile([P, 4, T], F32, name=f"x_raw{a}") for a in range(A)]
+        pieces = [((0, 256), (256, 384), (384, 512)), ((0, 256), (256, 512)), ((0, 256), (256, 512))]
+        x_raw = {
+            (a, t0): keep.tile([P, 4, t1 - t0], F32, name=f"x_raw{a}_{t0}") for a in range(A) for t0, t1 in pieces[a]
+        }
         x_bf = [keep.tile([P, T, 4], BF16, name=f"x_bf{a}", tag=f"share{a}", align_bytes=64) for a in range(A)]
         span = [1376, 1376, 704]
         codes = [keep.tile([P, span[a]], I32, name=f"codes{a}", align_bytes=64) for a in range(A)]
@@ -44,19 +48,18 @@ def tile_moe_tk_lin_relu2_kernel(
         b_t = keep.tile([P, E], F32, name="b_t")
         gate_t = keep.tile([P, TOP, T], F32, name="gate_t")
         y_t = keep.tile([P, SLOTS], F32, name="y_t")
-        prod = [keep.tile([P, T], F32, name=f"prod{r}") for r in range(TOP)]
-        sums = [keep.tile([P, T], F32, name=f"sums{r}") for r in range(3)]
+        ident = keep.tile([P, P], F32, name="ident")
         warm = keep.tile([P, 2], F32, name="warm")
 
         def x_rows(a):
             return xT[a * 512 : (a + 1) * 512, :].rearrange("(p j) t -> p j t", j=4)
 
         half = T // 2
-        nc.sync.dma_start(out=x_raw[0][:, :, 0:half], in_=x_rows(0)[:, :, 0:half])
-        nc.sync.dma_start(out=x_raw[0][:, :, half:T], in_=x_rows(0)[:, :, half:T])
-        nc.sync.dma_start(offs_t[:], offs)
-        nc.sync.dma_start(out=x_raw[1][:], in_=x_rows(1))
-        nc.sync.dma_start(out=x_raw[2][:], in_=x_rows(2))
+        for a in range(A):
+            for t0, t1 in pieces[a]:
+                nc.sync.dma_start(out=x_raw[(a, t0)][:], in_=x_rows(a)[:, :, t0:t1])
+            if a == 0:
+                nc.sync.dma_start(offs_t[:], offs)
 
         w_rows = w_words.rearrange("e a p c -> p (e a) c")
         ws_rows = w_scales.rearrange("e a q n -> q (e a) n")
@@ -71,6 +74,7 @@ def tile_moe_tk_lin_relu2_kernel(
         for r, pos in enumerate((pos1, pos2, pos3, pos4)):
             nc.sync.dma_start(pos_t[r][:], pos)
         nc.sync.dma_start(out=gate_t[:], in_=gate.rearrange("r p t -> p r t"))
+        make_identity(nc, ident[:])
 
         nc.vector.memset(warm[:, 0:1], 0.0)
         nc.scalar.activation(warm[:, 1:2], warm[:, 0:1], ACT.Relu)
@@ -81,7 +85,11 @@ def tile_moe_tk_lin_relu2_kernel(
             nc.gpsimd.memset(slot_planes[a][:].bitcast(I32), 0)
 
         def interleave(copy, a, t0, t1):
-            copy(x_bf[a][:, t0:t1, :], x_raw[a][:, :, t0:t1].rearrange("p j t -> p t j"))
+            base = max(p0 for p0, p1 in pieces[a] if p0 <= t0)
+            copy(
+                x_bf[a][:, t0:t1, :].rearrange("p (c i) j -> p c j i", i=4),
+                x_raw[(a, base)][:, :, t0 - base : t1 - base].rearrange("p j (c i) -> p c j i", i=4),
+            )
 
         def quantise(a, t0, t1):
             nc.vector.quantize_mx(
@@ -138,18 +146,24 @@ def tile_moe_tk_lin_relu2_kernel(
             for e in es:
                 nc.scalar.activation(y_t[:, e * C : (e + 1) * C], rels[e][:], ACT.Square)
 
-        interleave(nc.vector.tensor_copy, 0, 0, 256)
+        interleave(nc.vector.tensor_copy, 0, 0, 192)
+        interleave(nc.scalar.copy, 0, 192, 256)
         quantise(0, 0, 256)
-        interleave(nc.scalar.copy, 0, 432, 512)
-        interleave(nc.vector.tensor_copy, 0, 256, 432)
-        quantise(0, 256, 512)
+        interleave(nc.scalar.copy, 0, 256, 384)
+        interleave(nc.vector.tensor_copy, 0, 384, 512)
+        quantise(0, 256, 384)
+        quantise(0, 384, 512)
         gather_words(0, 0, 1024)
-        interleave(nc.scalar.copy, 1, 0, 512)
-        gather_words(0, 1024, 2048)
+        for t0, t1 in pieces[1]:
+            interleave(nc.scalar.copy, 1, t0, t1)
+        gather_words(0, 1024, 1792)
         quantise(1, 0, 512)
-        interleave(nc.scalar.copy, 2, 0, 512)
-        gather_words(1, 0, 1024)
+        gather_words(0, 1792, 2048)
+        for t0, t1 in pieces[2]:
+            interleave(nc.scalar.copy, 2, t0, t1)
+        gather_words(1, 0, 768)
         quantise(2, 0, 512)
+        gather_words(1, 768, 1024)
         gather_bytes(0, 1024)
         gather_bytes(1024, 2048)
         for e in range(4):
@@ -198,22 +212,51 @@ def tile_moe_tk_lin_relu2_kernel(
         for h in range(2):
             nc.vector.tensor_tensor(y_t[:, 7 * C + h * N : 7 * C + (h + 1) * N], rel7[h][:], rel7[h][:], ALU.mult)
 
+        cut = 3 * P
+
         def fetch(r, t0, t1):
+            product = keep.tile([P, t1 - t0], F32, name=f"product{r}_{t0}")
             nc.vector.tensor_tensor(
-                prod[r][:, t0:t1],
+                product[:],
                 y_t[:].indirect(pos_t[r][:, t0 // 16 : t1 // 16]),
                 gate_t[:, r, t0:t1],
                 ALU.mult,
             )
+            return product
 
-        fetch(0, 0, T)
-        fetch(1, 0, T)
-        fetch(2, 0, T)
-        nc.vector.tensor_tensor(sums[0][:], prod[0][:], prod[1][:], ALU.add)
-        fetch(3, 0, T)
-        halves = (slice(0, half), slice(half, T))
-        for cols in halves:
-            nc.vector.tensor_tensor(sums[1][:, cols], sums[0][:, cols], prod[2][:, cols], ALU.add)
-        for cols in halves:
-            nc.vector.tensor_tensor(sums[2][:, cols], sums[1][:, cols], prod[3][:, cols], ALU.add)
-            nc.sync.dma_start(out=out[:, cols], in_=sums[2][:, cols])
+        turned = [psum.tile([P, 512], F32, name="acc") for blk in range(T // P)]
+
+        def turn(product, blk, first, last):
+            nc.tensor.matmul(
+                turned[blk][:, 0:P], product[:, blk * P : (blk + 1) * P], ident[:], start=first, stop=last, is_transpose=True
+            )
+
+        def turn_back(blocks):
+            partial = psum.tile([P, 512], F32, name="acc")
+            for i, blk in enumerate(blocks):
+                staged = keep.tile([P, P], F32, name=f"staged{blk}")
+                nc.scalar.copy(staged[:], turned[blk][:, 0:P])
+                nc.tensor.transpose(partial[:, i * P : (i + 1) * P], staged[:], ident[:])
+            return partial
+
+        for r in range(2):
+            product = fetch(r, 0, T)
+            for blk in (3, 0, 1, 2):
+                turn(product, blk, r == 0, r == 1 and blk == 3)
+        partial_b = turn_back((3,))
+        product = fetch(2, 0, cut)
+        for blk in range(3):
+            turn(product, blk, False, True)
+        partial_a = turn_back((0, 1, 2))
+        third_b = fetch(2, cut, T)
+        fourth_b = fetch(3, cut, T)
+        sum_b = keep.tile([P, T - cut], F32, name="sum_b")
+        nc.vector.tensor_tensor(sum_b[:], partial_b[:, 0 : T - cut], third_b[:], ALU.add)
+        fourth_a = fetch(3, 0, cut)
+        result_b = keep.tile([P, T - cut], F32, name="result_b")
+        nc.vector.tensor_tensor(result_b[:], sum_b[:], fourth_b[:], ALU.add)
+        nc.sync.dma_start(out=out[:, cut:T], in_=result_b[:])
+        result_a = keep.tile([P, cut], F32, name="result_a")
+        for cols in (slice(0, 2 * P), slice(2 * P, cut)):
+            nc.vector.tensor_tensor(result_a[:, cols], partial_a[:, cols], fourth_a[:, cols], ALU.add)
+            nc.sync.dma_start(out=out[:, cols], in_=result_a[:, cols])

@@ -40,13 +40,12 @@ def tile_moe_tk_lin_relu2_kernel(
         x_bf = [keep.tile([P, T, 4], BF16, name=f"x_bf{a}", tag=f"share{a}", align_bytes=64) for a in range(A)]
         span = [1376, 1376, 704]
         codes = [keep.tile([P, span[a]], I32, name=f"codes{a}", align_bytes=64) for a in range(A)]
-        planes = keep.tile([P, 1376], U8, name="planes", align_bytes=64)
+        planes = keep.tile([P, 1376], U8, name="planes", tag="planes", align_bytes=64)
         slot_codes = [[None, None], [None, None], [None, None]]
         slot_planes = [keep.tile([P, SLOTS], U8, name=f"slot_planes{a}", align_bytes=64) for a in range(A)]
         w_t = keep.tile([P, E * A, 2 * N], U8, name="w_t", align_bytes=64)
         ws_t = keep.tile([P, E * A, N], U8, name="ws_t", align_bytes=64)
         b_t = keep.tile([P, E], F32, name="b_t")
-        gate_t = keep.tile([P, TOP, T], F32, name="gate_t")
         y_t = keep.tile([P, SLOTS], F32, name="y_t")
         ident = keep.tile([P, P], F32, name="ident")
         warm = keep.tile([P, 2], F32, name="warm")
@@ -73,7 +72,6 @@ def tile_moe_tk_lin_relu2_kernel(
         nc.sync.dma_start(out=b_t[:], in_=b)
         for r, pos in enumerate((pos1, pos2, pos3, pos4)):
             nc.sync.dma_start(pos_t[r][:], pos)
-        nc.sync.dma_start(out=gate_t[:], in_=gate.rearrange("r p t -> p r t"))
         make_identity(nc, ident[:])
 
         nc.vector.memset(warm[:, 0:1], 0.0)
@@ -166,6 +164,8 @@ def tile_moe_tk_lin_relu2_kernel(
         gather_words(1, 768, 1024)
         gather_bytes(0, 1024)
         gather_bytes(1024, 2048)
+        gate_t = keep.tile([P, TOP, T], F32, name="gate_t", tag="planes", align_bytes=64)
+        nc.sync.dma_start(out=gate_t[:], in_=gate.rearrange("r p t -> p r t"))
         for e in range(4):
             open_bank(e)
             multiply(e, 0, (0,))

@@ -38,8 +38,9 @@ def tile_moe_tk_lin_relu2_kernel(
             (a, t0): keep.tile([P, 4, t1 - t0], F32, name=f"x_raw{a}_{t0}") for a in range(A) for t0, t1 in pieces[a]
         }
         x_bf = [keep.tile([P, T, 4], BF16, name=f"x_bf{a}", tag=f"share{a}", align_bytes=64) for a in range(A)]
-        span = [1376, 1376, 704]
-        codes = [keep.tile([P, span[a]], I32, name=f"codes{a}", align_bytes=64) for a in range(A)]
+        span = [1376, 1024, 704]
+        all_codes = keep.tile([P, (A - 1) * T + span[0]], I32, name="all_codes", align_bytes=64)
+        codes = [all_codes[:, (A - 1 - a) * T : (A - 1 - a) * T + span[a]] for a in range(A)]
         planes = keep.tile([P, 1376], U8, name="planes", tag="planes", align_bytes=64)
         slot_codes = [[None, None], [None, None], [None, None]]
         slot_planes = [keep.tile([P, SLOTS], U8, name=f"slot_planes{a}", align_bytes=64) for a in range(A)]
@@ -77,10 +78,9 @@ def tile_moe_tk_lin_relu2_kernel(
         nc.vector.memset(warm[:, 0:1], 0.0)
         nc.scalar.activation(warm[:, 1:2], warm[:, 0:1], ACT.Relu)
         nc.vector.memset(planes[:].bitcast(I32), 0)
-        for a in range(A):
-            nc.vector.memset(codes[a][:, T:], 0)
+        nc.vector.memset(all_codes[:, A * T :], 0)
         for a in (1, 2):
-            nc.gpsimd.memset(slot_planes[a][:].bitcast(I32), 0)
+            nc.vector.memset(slot_planes[a][:].bitcast(I32), 0)
 
         def interleave(copy, a, t0, t1):
             base = max(p0 for p0, p1 in pieces[a] if p0 <= t0)
@@ -103,7 +103,7 @@ def tile_moe_tk_lin_relu2_kernel(
                 slot_codes[a][i] = keep.tile([P, 1024], I32, name=f"slot_codes{a}_{i}", tag=tag, align_bytes=64)
             nc.vector.tensor_copy(
                 slot_codes[a][i][:, s0 - 1024 * i : s1 - 1024 * i].bitcast(U32),
-                codes[a][:].bitcast(U32).indirect(offs_t[:, s0 // 16 : s1 // 16]),
+                codes[a].bitcast(U32).indirect(offs_t[:, s0 // 16 : s1 // 16]),
             )
 
         def gather_bytes(s0, s1):
@@ -169,6 +169,17 @@ def tile_moe_tk_lin_relu2_kernel(
         for e in range(4):
             open_bank(e)
             multiply(e, 0, (0,))
+        idle_bank = psum.tile([P, 512], F32, name="acc")
+        for n in range(3):
+            nc.tensor.matmul_mx(
+                out=idle_bank[:],
+                lhsT=w_t[:, 0, :].bitcast(FP4X4),
+                lhsT_scale=ws_t[:, 0, :],
+                rhs=slot_codes[0][0][:, 0:512].bitcast(FP8X4),
+                rhs_scale=slot_planes[0][:, 0:512],
+                start=True,
+                stop=True,
+            )
         for e in range(4):
             multiply(e, 0, (1,))
         rel_pair = [keep.tile([P, 2 * C], F32, name=f"rel_pair{i}") for i in range(2)]

@@ -29,7 +29,7 @@ def tile_moe_tk_lin_relu2_kernel(
     with ExitStack() as ctx:
         keep = ctx.enter_context(tc.tile_pool(name="keep", bufs=1))
         ring = ctx.enter_context(tc.tile_pool(name="ring", bufs=3))
-        psum = ctx.enter_context(tc.psum_pool(name="psum", bufs=8))
+        psum = ctx.enter_context(tc.psum_pool(name="psum", bufs=1))
 
         offs_t = keep.tile([P, SLOTS // 16], U16, name="offs_t")
         pos_t = [keep.tile([P, T // 16], U16, name=f"pos_t{r}") for r in range(TOP)]
@@ -131,7 +131,8 @@ def tile_moe_tk_lin_relu2_kernel(
                 )
 
         def open_bank(e):
-            bank = psum.tile([P, 512], F32, name="acc")
+            tag = ("bank0", "bank1", "even", "odd", "even", "odd", "even")[e]
+            bank = psum.tile([P, 1024 if tag == "odd" else 512], F32, name=f"acc{e}", tag=tag)
             for h in range(2):
                 acc[(e, h)] = bank[:, h * N : (h + 1) * N]
             acc[e] = bank
@@ -169,20 +170,9 @@ def tile_moe_tk_lin_relu2_kernel(
         for e in range(4):
             open_bank(e)
             multiply(e, 0, (0,))
-        idle_bank = psum.tile([P, 512], F32, name="acc")
-        for n in range(3):
-            nc.tensor.matmul_mx(
-                out=idle_bank[:],
-                lhsT=w_t[:, 0, :].bitcast(FP4X4),
-                lhsT_scale=ws_t[:, 0, :],
-                rhs=slot_codes[0][0][:, 0:512].bitcast(FP8X4),
-                rhs_scale=slot_planes[0][:, 0:512],
-                start=True,
-                stop=True,
-            )
         for e in range(4):
             multiply(e, 0, (1,))
-        rel_pair = [keep.tile([P, 2 * C], F32, name=f"rel_pair{i}") for i in range(2)]
+        rel_pair = [keep.tile([P, 2 * C], F32, name=f"rel_pair{i}") for i in range(3)]
         for i in range(2):
             gather_words(2, 512 * i, 512 * i + 512)
             for e in (2 * i, 2 * i + 1):
@@ -192,9 +182,8 @@ def tile_moe_tk_lin_relu2_kernel(
             nc.scalar.activation(
                 rel_pair[e // 2][:, (e % 2) * C : (e % 2 + 1) * C], acc[e][:, 0:C], ACT.Relu, bias=b_t[:, e : e + 1]
             )
-            if e >= 2:
-                i = e - 2
-                nc.scalar.activation(y_t[:, 512 * i : 512 * i + 512], rel_pair[i][:], ACT.Square)
+        for i in range(2):
+            nc.scalar.activation(y_t[:, 512 * i : 512 * i + 512], rel_pair[i][:], ACT.Square)
         gather_words(1, 1024, 1536)
         for e in (4, 5):
             open_bank(e)
@@ -203,18 +192,24 @@ def tile_moe_tk_lin_relu2_kernel(
         for e in (4, 5):
             multiply(e, 0, (2,))
             multiply(e, 1, (0, 1, 2))
-        finish((4, 5))
-        gather_words(1, 1536, 2048)
+        for e in (4, 5):
+            nc.scalar.activation(
+                rel_pair[2][:, (e % 2) * C : (e % 2 + 1) * C], acc[e][:, 0:C], ACT.Relu, bias=b_t[:, e : e + 1]
+            )
+        gather_words(1, 1536, 1792)
         open_bank(6)
         multiply(6, 0, (0, 1))
-        for h in range(2):
-            acc[(7, h)] = psum.tile([P, 512], F32, name="acc")[:, 0:N]
-            multiply(7, h, (0, 1))
         gather_words(2, 1536, 1792)
         multiply(6, 0, (2,))
         multiply(6, 1, (0, 1, 2))
         finish((6,))
+        gather_words(1, 1792, 2048)
+        last_banks = psum.tile([P, 1024], F32, name="acc7", tag="odd")
+        for h in range(2):
+            acc[(7, h)] = last_banks[:, 512 * h : 512 * h + N]
+            multiply(7, h, (0, 1))
         gather_words(2, 1792, 2048)
+        nc.vector.tensor_tensor(y_t[:, 4 * C : 6 * C], rel_pair[2][:], rel_pair[2][:], ALU.mult)
         for h in range(2):
             multiply(7, h, (2,))
         rel7 = [keep.tile([P, N], F32, name=f"rel7_{h}") for h in range(2)]
@@ -223,7 +218,7 @@ def tile_moe_tk_lin_relu2_kernel(
         for h in range(2):
             nc.vector.tensor_tensor(y_t[:, 7 * C + h * N : 7 * C + (h + 1) * N], rel7[h][:], rel7[h][:], ALU.mult)
 
-        cut = 3 * P
+        cut = 2 * P
 
         def fetch(r, t0, t1):
             product = keep.tile([P, t1 - t0], F32, name=f"product{r}_{t0}")
@@ -235,15 +230,16 @@ def tile_moe_tk_lin_relu2_kernel(
             )
             return product
 
-        turned = [psum.tile([P, 512], F32, name="acc") for blk in range(T // P)]
+        turned = [psum.tile([P, 512], F32, name=f"turned{blk}") for blk in range(3)]
+        turned.append(psum.tile([P, 512], F32, name="turned3", tag="bank0"))
 
         def turn(product, blk, first, last):
             nc.tensor.matmul(
                 turned[blk][:, 0:P], product[:, blk * P : (blk + 1) * P], ident[:], start=first, stop=last, is_transpose=True
             )
 
-        def turn_back(blocks):
-            partial = psum.tile([P, 512], F32, name="acc")
+        def turn_back(blocks, tag):
+            partial = psum.tile([P, 512], F32, name=f"partial{blocks[0]}", tag=tag)
             for i, blk in enumerate(blocks):
                 staged = keep.tile([P, P], F32, name=f"staged{blk}")
                 nc.scalar.copy(staged[:], turned[blk][:, 0:P])
@@ -252,22 +248,21 @@ def tile_moe_tk_lin_relu2_kernel(
 
         for r in range(2):
             product = fetch(r, 0, T)
-            for blk in (3, 0, 1, 2):
-                turn(product, blk, r == 0, r == 1 and blk == 3)
-        partial_b = turn_back((3,))
+            for blk in (2, 3, 0, 1):
+                turn(product, blk, r == 0, r == 1 and blk >= 2)
+        partial_b = turn_back((2, 3), "bank1")
         product = fetch(2, 0, cut)
-        for blk in range(3):
+        for blk in range(2):
             turn(product, blk, False, True)
-        partial_a = turn_back((0, 1, 2))
+        partial_a = turn_back((0, 1), "even")
         third_b = fetch(2, cut, T)
         fourth_b = fetch(3, cut, T)
+        fourth_a = fetch(3, 0, cut)
         sum_b = keep.tile([P, T - cut], F32, name="sum_b")
         nc.vector.tensor_tensor(sum_b[:], partial_b[:, 0 : T - cut], third_b[:], ALU.add)
-        fourth_a = fetch(3, 0, cut)
+        result_a = keep.tile([P, cut], F32, name="result_a")
+        nc.vector.tensor_tensor(result_a[:], partial_a[:, 0:cut], fourth_a[:], ALU.add)
+        nc.sync.dma_start(out=out[:, 0:cut], in_=result_a[:])
         result_b = keep.tile([P, T - cut], F32, name="result_b")
         nc.vector.tensor_tensor(result_b[:], sum_b[:], fourth_b[:], ALU.add)
         nc.sync.dma_start(out=out[:, cut:T], in_=result_b[:])
-        result_a = keep.tile([P, cut], F32, name="result_a")
-        for cols in (slice(0, 2 * P), slice(2 * P, cut)):
-            nc.vector.tensor_tensor(result_a[:, cols], partial_a[:, cols], fourth_a[:, cols], ALU.add)
-            nc.sync.dma_start(out=out[:, cols], in_=result_a[:, cols])

@@ -28,21 +28,21 @@ def tile_moe_tk_lin_relu2_kernel(
     nc = tc.nc
     with ExitStack() as ctx:
         keep = ctx.enter_context(tc.tile_pool(name="keep", bufs=1))
-        ring = ctx.enter_context(tc.tile_pool(name="ring", bufs=3))
         psum = ctx.enter_context(tc.psum_pool(name="psum", bufs=1))
 
         offs_t = keep.tile([P, SLOTS // 16], U16, name="offs_t")
         pos_t = [keep.tile([P, T // 16], U16, name=f"pos_t{r}") for r in range(TOP)]
         pieces = [((0, 256), (256, 384), (384, 512)), ((0, 256), (256, 512)), ((0, 256), (256, 512))]
         x_raw = {
-            (a, t0): keep.tile([P, 4, t1 - t0], F32, name=f"x_raw{a}_{t0}") for a in range(A) for t0, t1 in pieces[a]
+            (a, t0): keep.tile([P, 4, t1 - t0], F32, name=f"x_raw{a}_{t0}", tag=f"raw{a}_{t0}", align_bytes=64)
+            for a in range(A)
+            for t0, t1 in pieces[a]
         }
         x_bf = [keep.tile([P, T, 4], BF16, name=f"x_bf{a}", tag=f"share{a}", align_bytes=64) for a in range(A)]
-        span = [1376, 1024, 704]
-        all_codes = keep.tile([P, (A - 1) * T + span[0]], I32, name="all_codes", align_bytes=64)
-        codes = [all_codes[:, (A - 1 - a) * T : (A - 1 - a) * T + span[a]] for a in range(A)]
+        all_codes = keep.tile([P, (A - 1) * T + 1376], I32, name="all_codes", align_bytes=64)
+        codes = [all_codes[:, (A - 1 - a) * T : (A - 1 - a) * T + 1376] for a in range(A)]
         planes = keep.tile([P, 1376], U8, name="planes", tag="planes", align_bytes=64)
-        slot_codes = [[None, None], [None, None], [None, None]]
+        slot_codes = {}
         slot_planes = [keep.tile([P, SLOTS], U8, name=f"slot_planes{a}", align_bytes=64) for a in range(A)]
         w_t = keep.tile([P, E * A, 2 * N], U8, name="w_t", align_bytes=64)
         ws_t = keep.tile([P, E * A, N], U8, name="ws_t", align_bytes=64)
@@ -54,7 +54,6 @@ def tile_moe_tk_lin_relu2_kernel(
         def x_rows(a):
             return xT[a * 512 : (a + 1) * 512, :].rearrange("(p j) t -> p j t", j=4)
 
-        half = T // 2
         for a in range(A):
             for t0, t1 in pieces[a]:
                 nc.sync.dma_start(out=x_raw[(a, t0)][:], in_=x_rows(a)[:, :, t0:t1])
@@ -96,14 +95,17 @@ def tile_moe_tk_lin_relu2_kernel(
                 in_=x_bf[a][:, t0:t1, :].rearrange("p t j -> p (t j)"),
             )
 
-        def gather_words(a, s0, s1):
-            i = s0 // 1024
-            if slot_codes[a][i] is None:
-                tag = "share2" if (a, i) == (1, 1) else f"slot_codes{a}_{i}"
-                slot_codes[a][i] = keep.tile([P, 1024], I32, name=f"slot_codes{a}_{i}", tag=tag, align_bytes=64)
+        def gather_words(a, s0, s1, tag=None, words=None):
+            if words is None:
+                words = keep.tile(
+                    [P, s1 - s0], I32, name=f"slot_codes{a}_{s0}", tag=tag or f"slot_codes{a}_{s0}", align_bytes=64
+                )[:]
+            for s in range(s0, s1, N):
+                slot_codes[(a, s)] = words[:, s - s0 : s - s0 + N]
+            width = 1376 if s1 - s0 > 512 else 704
             nc.vector.tensor_copy(
-                slot_codes[a][i][:, s0 - 1024 * i : s1 - 1024 * i].bitcast(U32),
-                codes[a].bitcast(U32).indirect(offs_t[:, s0 // 16 : s1 // 16]),
+                words.bitcast(U32),
+                codes[a][:, 0:width].bitcast(U32).indirect(offs_t[:, s0 // 16 : s1 // 16]),
             )
 
         def gather_bytes(s0, s1):
@@ -124,26 +126,17 @@ def tile_moe_tk_lin_relu2_kernel(
                     out=acc[(e, h)],
                     lhsT=w_t[:, e * A + a, :].bitcast(FP4X4),
                     lhsT_scale=ws_t[:, e * A + a, :],
-                    rhs=slot_codes[a][e // 4][:, (e % 4) * C + h * N : (e % 4) * C + h * N + N].bitcast(FP8X4),
+                    rhs=slot_codes[(a, e * C + h * N)].bitcast(FP8X4),
                     rhs_scale=slot_planes[a][:, cols],
                     start=(a == 0),
                     stop=(a == A - 1),
                 )
 
         def open_bank(e):
-            tag = ("bank0", "bank1", "even", "odd", "even", "odd", "even")[e]
-            bank = psum.tile([P, 1024 if tag == "odd" else 512], F32, name=f"acc{e}", tag=tag)
+            bank = psum.tile([P, 512], F32, name=f"acc{e}", tag=f"bank{e}")
             for h in range(2):
                 acc[(e, h)] = bank[:, h * N : (h + 1) * N]
             acc[e] = bank
-
-        def finish(es):
-            rels = {}
-            for e in es:
-                rels[e] = ring.tile([P, C], F32, name="rel")
-                nc.scalar.activation(rels[e][:], acc[e][:, 0:C], ACT.Relu, bias=b_t[:, e : e + 1])
-            for e in es:
-                nc.scalar.activation(y_t[:, e * C : (e + 1) * C], rels[e][:], ACT.Square)
 
         interleave(nc.vector.tensor_copy, 0, 0, 192)
         interleave(nc.scalar.copy, 0, 192, 256)
@@ -155,14 +148,14 @@ def tile_moe_tk_lin_relu2_kernel(
         gather_words(0, 0, 1024)
         for t0, t1 in pieces[1]:
             interleave(nc.scalar.copy, 1, t0, t1)
-        gather_words(0, 1024, 1792)
+        gather_words(0, 1024, 1920)
         quantise(1, 0, 512)
-        gather_words(0, 1792, 2048)
+        gather_words(0, 1920, 2048, tag="raw1_256")
         for t0, t1 in pieces[2]:
             interleave(nc.scalar.copy, 2, t0, t1)
-        gather_words(1, 0, 768)
+        gather_words(1, 0, 896)
         quantise(2, 0, 512)
-        gather_words(1, 768, 1024)
+        gather_words(1, 896, 1024, tag="raw2_256")
         gather_bytes(0, 1024)
         gather_bytes(1024, 2048)
         gate_t = keep.tile([P, TOP, T], F32, name="gate_t", tag="planes", align_bytes=64)
@@ -173,18 +166,22 @@ def tile_moe_tk_lin_relu2_kernel(
         for e in range(4):
             multiply(e, 0, (1,))
         rel_pair = [keep.tile([P, 2 * C], F32, name=f"rel_pair{i}") for i in range(3)]
-        for i in range(2):
-            gather_words(2, 512 * i, 512 * i + 512)
-            for e in (2 * i, 2 * i + 1):
-                multiply(e, 0, (2,))
-                multiply(e, 1, (0, 1, 2))
-        for e in range(4):
+
+        def relu(e):
             nc.scalar.activation(
                 rel_pair[e // 2][:, (e % 2) * C : (e % 2 + 1) * C], acc[e][:, 0:C], ACT.Relu, bias=b_t[:, e : e + 1]
             )
+
+        gather_words(2, 0, 1024)
+        for e in range(4):
+            multiply(e, 0, (2,))
+            multiply(e, 1, (0, 1, 2))
+        for e in range(4):
+            relu(e)
         for i in range(2):
             nc.scalar.activation(y_t[:, 512 * i : 512 * i + 512], rel_pair[i][:], ACT.Square)
-        gather_words(1, 1024, 1536)
+        late_words = keep.tile([P, 1024], I32, name="late_words", tag="share2", align_bytes=64)
+        gather_words(1, 1024, 1536, words=late_words[:, 0:512])
         for e in (4, 5):
             open_bank(e)
             multiply(e, 0, (0, 1))
@@ -193,23 +190,22 @@ def tile_moe_tk_lin_relu2_kernel(
             multiply(e, 0, (2,))
             multiply(e, 1, (0, 1, 2))
         for e in (4, 5):
-            nc.scalar.activation(
-                rel_pair[2][:, (e % 2) * C : (e % 2 + 1) * C], acc[e][:, 0:C], ACT.Relu, bias=b_t[:, e : e + 1]
-            )
-        gather_words(1, 1536, 1792)
+            relu(e)
+        nc.scalar.activation(y_t[:, 4 * C : 6 * C], rel_pair[2][:], ACT.Square)
+        gather_words(1, 1536, 2048, words=late_words[:, 512:1024])
         open_bank(6)
         multiply(6, 0, (0, 1))
+        for h, tag in enumerate(("bank7", "bank0")):
+            bank = psum.tile([P, 512], F32, name=f"acc7_{h}", tag=tag)
+            acc[(7, h)] = bank[:, 0:N]
+            multiply(7, h, (0, 1))
         gather_words(2, 1536, 1792)
         multiply(6, 0, (2,))
         multiply(6, 1, (0, 1, 2))
-        finish((6,))
-        gather_words(1, 1792, 2048)
-        last_banks = psum.tile([P, 1024], F32, name="acc7", tag="odd")
-        for h in range(2):
-            acc[(7, h)] = last_banks[:, 512 * h : 512 * h + N]
-            multiply(7, h, (0, 1))
+        rel6 = keep.tile([P, C], F32, name="rel6")
+        nc.scalar.activation(rel6[:], acc[6][:, 0:C], ACT.Relu, bias=b_t[:, 6:7])
+        nc.scalar.activation(y_t[:, 6 * C : 7 * C], rel6[:], ACT.Square)
         gather_words(2, 1792, 2048)
-        nc.vector.tensor_tensor(y_t[:, 4 * C : 6 * C], rel_pair[2][:], rel_pair[2][:], ALU.mult)
         for h in range(2):
             multiply(7, h, (2,))
         rel7 = [keep.tile([P, N], F32, name=f"rel7_{h}") for h in range(2)]
@@ -230,8 +226,7 @@ def tile_moe_tk_lin_relu2_kernel(
             )
             return product
 
-        turned = [psum.tile([P, 512], F32, name=f"turned{blk}") for blk in range(3)]
-        turned.append(psum.tile([P, 512], F32, name="turned3", tag="bank0"))
+        turned = [psum.tile([P, 512], F32, name=f"turned{blk}", tag=f"bank{blk + 1}") for blk in range(4)]
 
         def turn(product, blk, first, last):
             nc.tensor.matmul(
@@ -241,7 +236,7 @@ def tile_moe_tk_lin_relu2_kernel(
         def turn_back(blocks, tag):
             partial = psum.tile([P, 512], F32, name=f"partial{blocks[0]}", tag=tag)
             for i, blk in enumerate(blocks):
-                staged = keep.tile([P, P], F32, name=f"staged{blk}")
+                staged = keep.tile([P, P], F32, name=f"staged{blk}", tag=f"staged{blk}")
                 nc.scalar.copy(staged[:], turned[blk][:, 0:P])
                 nc.tensor.transpose(partial[:, i * P : (i + 1) * P], staged[:], ident[:])
             return partial
@@ -250,19 +245,18 @@ def tile_moe_tk_lin_relu2_kernel(
             product = fetch(r, 0, T)
             for blk in (2, 3, 0, 1):
                 turn(product, blk, r == 0, r == 1 and blk >= 2)
-        partial_b = turn_back((2, 3), "bank1")
+        partial_b = turn_back((2, 3), "bank5")
         product = fetch(2, 0, cut)
         for blk in range(2):
             turn(product, blk, False, True)
-        partial_a = turn_back((0, 1), "even")
+        partial_a = turn_back((0, 1), "bank6")
         third_b = fetch(2, cut, T)
-        fourth_b = fetch(3, cut, T)
-        fourth_a = fetch(3, 0, cut)
+        fourth = fetch(3, 0, T)
         sum_b = keep.tile([P, T - cut], F32, name="sum_b")
         nc.vector.tensor_tensor(sum_b[:], partial_b[:, 0 : T - cut], third_b[:], ALU.add)
         result_a = keep.tile([P, cut], F32, name="result_a")
-        nc.vector.tensor_tensor(result_a[:], partial_a[:, 0:cut], fourth_a[:], ALU.add)
+        nc.vector.tensor_tensor(result_a[:], partial_a[:, 0:cut], fourth[:, 0:cut], ALU.add)
         nc.sync.dma_start(out=out[:, 0:cut], in_=result_a[:])
-        result_b = keep.tile([P, T - cut], F32, name="result_b")
-        nc.vector.tensor_tensor(result_b[:], sum_b[:], fourth_b[:], ALU.add)
+        result_b = keep.tile([P, T - cut], F32, name="result_b", tag="staged1")
+        nc.vector.tensor_tensor(result_b[:], sum_b[:], fourth[:, cut:T], ALU.add)
         nc.sync.dma_start(out=out[:, cut:T], in_=result_b[:])

@@ -43,12 +43,11 @@ def tile_moe_tk_lin_relu2_kernel(
         codes = [all_codes[:, (A - 1 - a) * T : (A - 1 - a) * T + 1376] for a in range(A)]
         planes = keep.tile([P, 1376], U8, name="planes", tag="planes", align_bytes=64)
         slot_codes = {}
-        slot_planes = [keep.tile([P, SLOTS], U8, name=f"slot_planes{a}", align_bytes=64) for a in range(A)]
+        gathered_planes = keep.tile([P, SLOTS], U8, name="gathered_planes", align_bytes=64)
         w_t = keep.tile([P, E * A, 2 * N], U8, name="w_t", align_bytes=64)
         ws_t = keep.tile([P, E * A, N], U8, name="ws_t", align_bytes=64)
         b_t = keep.tile([P, E], F32, name="b_t")
         y_t = keep.tile([P, SLOTS], F32, name="y_t")
-        ident = keep.tile([P, P], F32, name="ident")
         warm = keep.tile([P, 2], F32, name="warm")
 
         def x_rows(a):
@@ -72,14 +71,11 @@ def tile_moe_tk_lin_relu2_kernel(
         nc.sync.dma_start(out=b_t[:], in_=b)
         for r, pos in enumerate((pos1, pos2, pos3, pos4)):
             nc.sync.dma_start(pos_t[r][:], pos)
-        make_identity(nc, ident[:])
 
         nc.vector.memset(warm[:, 0:1], 0.0)
         nc.scalar.activation(warm[:, 1:2], warm[:, 0:1], ACT.Relu)
         nc.vector.memset(planes[:].bitcast(I32), 0)
         nc.vector.memset(all_codes[:, A * T :], 0)
-        for a in (1, 2):
-            nc.vector.memset(slot_planes[a][:].bitcast(I32), 0)
 
         def interleave(copy, a, t0, t1):
             base = max(p0 for p0, p1 in pieces[a] if p0 <= t0)
@@ -145,11 +141,16 @@ def tile_moe_tk_lin_relu2_kernel(
         interleave(nc.vector.tensor_copy, 0, 384, 512)
         quantise(0, 256, 384)
         quantise(0, 384, 512)
+        moved_planes = keep.tile([P, 2 * SLOTS], U8, name="moved_planes", tag="share0", align_bytes=64)
+        nc.gpsimd.memset(moved_planes[:].bitcast(I32), 0)
+        slot_planes = [gathered_planes[:], moved_planes[:, 0:SLOTS], moved_planes[:, SLOTS : 2 * SLOTS]]
         gather_words(0, 0, 1024)
         for t0, t1 in pieces[1]:
             interleave(nc.scalar.copy, 1, t0, t1)
         gather_words(0, 1024, 1920)
         quantise(1, 0, 512)
+        ident = keep.tile([P, P], F32, name="ident", tag="share1", align_bytes=64)
+        make_identity(nc, ident[:])
         gather_words(0, 1920, 2048, tag="raw1_256")
         for t0, t1 in pieces[2]:
             interleave(nc.scalar.copy, 2, t0, t1)

@@ -129,7 +129,8 @@ def tile_moe_tk_lin_relu2_kernel(
                 )
 
         def open_bank(e):
-            bank = psum.tile([P, 512], F32, name=f"acc{e}", tag=f"bank{e}")
+            tag = ("bank0", "bank1", "even", "odd", "even", "odd", "even")[e]
+            bank = psum.tile([P, 1024 if tag == "odd" else 512], F32, name=f"acc{e}", tag=tag)
             for h in range(2):
                 acc[(e, h)] = bank[:, h * N : (h + 1) * N]
             acc[e] = bank
@@ -167,18 +168,15 @@ def tile_moe_tk_lin_relu2_kernel(
         for e in range(4):
             multiply(e, 0, (1,))
         rel_pair = [keep.tile([P, 2 * C], F32, name=f"rel_pair{i}") for i in range(3)]
-
-        def relu(e):
+        for i in range(2):
+            gather_words(2, 512 * i, 512 * i + 512)
+            for e in (2 * i, 2 * i + 1):
+                multiply(e, 0, (2,))
+                multiply(e, 1, (0, 1, 2))
+        for e in range(4):
             nc.scalar.activation(
                 rel_pair[e // 2][:, (e % 2) * C : (e % 2 + 1) * C], acc[e][:, 0:C], ACT.Relu, bias=b_t[:, e : e + 1]
             )
-
-        gather_words(2, 0, 1024)
-        for e in range(4):
-            multiply(e, 0, (2,))
-            multiply(e, 1, (0, 1, 2))
-        for e in range(4):
-            relu(e)
         for i in range(2):
             nc.scalar.activation(y_t[:, 512 * i : 512 * i + 512], rel_pair[i][:], ACT.Square)
         late_words = keep.tile([P, 1024], I32, name="late_words", tag="share2", align_bytes=64)
@@ -191,22 +189,25 @@ def tile_moe_tk_lin_relu2_kernel(
             multiply(e, 0, (2,))
             multiply(e, 1, (0, 1, 2))
         for e in (4, 5):
-            relu(e)
-        nc.scalar.activation(y_t[:, 4 * C : 6 * C], rel_pair[2][:], ACT.Square)
-        gather_words(1, 1536, 2048, words=late_words[:, 512:1024])
+            nc.scalar.activation(
+                rel_pair[2][:, (e % 2) * C : (e % 2 + 1) * C], acc[e][:, 0:C], ACT.Relu, bias=b_t[:, e : e + 1]
+            )
+        gather_words(1, 1536, 1792, words=late_words[:, 512:768])
         open_bank(6)
         multiply(6, 0, (0, 1))
-        for h, tag in enumerate(("bank7", "bank0")):
-            bank = psum.tile([P, 512], F32, name=f"acc7_{h}", tag=tag)
-            acc[(7, h)] = bank[:, 0:N]
-            multiply(7, h, (0, 1))
         gather_words(2, 1536, 1792)
         multiply(6, 0, (2,))
         multiply(6, 1, (0, 1, 2))
         rel6 = keep.tile([P, C], F32, name="rel6")
         nc.scalar.activation(rel6[:], acc[6][:, 0:C], ACT.Relu, bias=b_t[:, 6:7])
         nc.scalar.activation(y_t[:, 6 * C : 7 * C], rel6[:], ACT.Square)
+        gather_words(1, 1792, 2048, words=late_words[:, 768:1024])
+        last_banks = psum.tile([P, 1024], F32, name="acc7", tag="odd")
+        for h in range(2):
+            acc[(7, h)] = last_banks[:, 512 * h : 512 * h + N]
+            multiply(7, h, (0, 1))
         gather_words(2, 1792, 2048)
+        nc.vector.tensor_tensor(y_t[:, 4 * C : 6 * C], rel_pair[2][:], rel_pair[2][:], ALU.mult)
         for h in range(2):
             multiply(7, h, (2,))
         rel7 = [keep.tile([P, N], F32, name=f"rel7_{h}") for h in range(2)]
@@ -227,7 +228,8 @@ def tile_moe_tk_lin_relu2_kernel(
             )
             return product
 
-        turned = [psum.tile([P, 512], F32, name=f"turned{blk}", tag=f"bank{blk + 1}") for blk in range(4)]
+        turned = [psum.tile([P, 512], F32, name=f"turned{blk}") for blk in range(3)]
+        turned.append(psum.tile([P, 512], F32, name="turned3", tag="bank0"))
 
         def turn(product, blk, first, last):
             nc.tensor.matmul(
@@ -246,11 +248,11 @@ def tile_moe_tk_lin_relu2_kernel(
             product = fetch(r, 0, T)
             for blk in (2, 3, 0, 1):
                 turn(product, blk, r == 0, r == 1 and blk >= 2)
-        partial_b = turn_back((2, 3), "bank5")
         product = fetch(2, 0, cut)
         for blk in range(2):
             turn(product, blk, False, True)
-        partial_a = turn_back((0, 1), "bank6")
+        partial_b = turn_back((2, 3), "bank1")
+        partial_a = turn_back((0, 1), "even")
         third_b = fetch(2, cut, T)
         fourth = fetch(3, 0, T)
         sum_b = keep.tile([P, T - cut], F32, name="sum_b")

@@ -28,6 +28,7 @@ def tile_moe_tk_lin_relu2_kernel(
     nc = tc.nc
     with ExitStack() as ctx:
         keep = ctx.enter_context(tc.tile_pool(name="keep", bufs=1))
+        reuse = ctx.enter_context(tc.tile_pool(name="reuse", bufs=1))
         psum = ctx.enter_context(tc.psum_pool(name="psum", bufs=1))
 
         offs_t = keep.tile([P, SLOTS // 16], U16, name="offs_t")
@@ -38,14 +39,14 @@ def tile_moe_tk_lin_relu2_kernel(
             for a in range(A)
             for t0, t1 in pieces[a]
         }
-        x_bf = [keep.tile([P, T, 4], BF16, name=f"x_bf{a}", tag=f"share{a}", align_bytes=64) for a in range(A)]
+        x_bf = [reuse.tile([P, T, 4], BF16, name="x_bf0", align_bytes=64, offset=1024)]
+        x_bf.extend(keep.tile([P, T, 4], BF16, name=f"x_bf{a}", tag=f"share{a}", align_bytes=64) for a in (1, 2))
         all_codes = keep.tile([P, (A - 1) * T + 1376], I32, name="all_codes", align_bytes=64)
         codes = [all_codes[:, (A - 1 - a) * T : (A - 1 - a) * T + 1376] for a in range(A)]
         planes = keep.tile([P, 1376], U8, name="planes", tag="planes", align_bytes=64)
         slot_codes = {}
         gathered_planes = keep.tile([P, SLOTS], U8, name="gathered_planes", align_bytes=64)
         w_t = keep.tile([P, E * A, 2 * N], U8, name="w_t", align_bytes=64)
-        ws_t = keep.tile([P, E * A, N], U8, name="ws_t", align_bytes=64)
         b_t = keep.tile([P, E], F32, name="b_t")
         y_t = keep.tile([P, SLOTS], F32, name="y_t")
         warm = keep.tile([P, 2], F32, name="warm")
@@ -61,13 +62,7 @@ def tile_moe_tk_lin_relu2_kernel(
 
         w_rows = w_words.rearrange("e a p c -> p (e a) c")
         ws_rows = w_scales.rearrange("e a q n -> q (e a) n")
-        nc.gpsimd.memset(ws_t[:].rearrange("p i n -> p (i n)").bitcast(I32), 0)
         nc.sync.dma_start(out=w_t[:].bitcast(I32), in_=w_rows.bitcast(I32))
-        for q in range(4):
-            nc.sync.dma_start(
-                out=ws_t[32 * q : 32 * q + 4, :, :].bitcast(I32),
-                in_=ws_rows[4 * q : 4 * q + 4, :, :].bitcast(I32),
-            )
         nc.sync.dma_start(out=b_t[:], in_=b)
         for r, pos in enumerate((pos1, pos2, pos3, pos4)):
             nc.sync.dma_start(pos_t[r][:], pos)
@@ -142,7 +137,14 @@ def tile_moe_tk_lin_relu2_kernel(
         interleave(nc.vector.tensor_copy, 0, 384, 512)
         quantise(0, 256, 384)
         quantise(0, 384, 512)
-        moved_planes = keep.tile([P, 2 * SLOTS], U8, name="moved_planes", tag="share0", align_bytes=64)
+        ws_t = reuse.tile([P, E * A, N], U8, name="ws_t", align_bytes=64, offset=0)
+        nc.gpsimd.memset(ws_t[:].rearrange("p i n -> p (i n)").bitcast(I32), 0)
+        for q in range(4):
+            nc.sync.dma_start(
+                out=ws_t[32 * q : 32 * q + 4, :, :].bitcast(I32),
+                in_=ws_rows[4 * q : 4 * q + 4, :, :].bitcast(I32),
+            )
+        moved_planes = reuse.tile([P, 2 * SLOTS], U8, name="moved_planes", align_bytes=64, offset=E * A * N)
         nc.gpsimd.memset(moved_planes[:].bitcast(I32), 0)
         slot_planes = [gathered_planes[:], moved_planes[:, 0:SLOTS], moved_planes[:, SLOTS : 2 * SLOTS]]
         gather_words(0, 0, 1024)
@@ -192,6 +194,7 @@ def tile_moe_tk_lin_relu2_kernel(
             nc.scalar.activation(
                 rel_pair[2][:, (e % 2) * C : (e % 2 + 1) * C], acc[e][:, 0:C], ACT.Relu, bias=b_t[:, e : e + 1]
             )
+        nc.scalar.activation(y_t[:, 5 * C : 6 * C], rel_pair[2][:, C : 2 * C], ACT.Square)
         gather_words(1, 1536, 1792, words=late_words[:, 512:768])
         open_bank(6)
         multiply(6, 0, (0, 1))
@@ -206,8 +209,9 @@ def tile_moe_tk_lin_relu2_kernel(
         for h in range(2):
             acc[(7, h)] = last_banks[:, 512 * h : 512 * h + N]
             multiply(7, h, (0, 1))
-        gather_words(2, 1792, 2048)
-        nc.vector.tensor_tensor(y_t[:, 4 * C : 6 * C], rel_pair[2][:], rel_pair[2][:], ALU.mult)
+        gather_words(2, 1792, 1920)
+        gather_words(2, 1920, 2048)
+        nc.vector.tensor_tensor(y_t[:, 4 * C : 5 * C], rel_pair[2][:, 0:C], rel_pair[2][:, 0:C], ALU.mult)
         for h in range(2):
             multiply(7, h, (2,))
         rel7 = [keep.tile([P, N], F32, name=f"rel7_{h}") for h in range(2)]

@@ -33,7 +33,7 @@ def tile_moe_tk_lin_relu2_kernel(
 
         offs_t = keep.tile([P, SLOTS // 16], U16, name="offs_t")
         pos_t = [keep.tile([P, T // 16], U16, name=f"pos_t{r}") for r in range(TOP)]
-        pieces = [((0, 256), (256, 384), (384, 512)), ((0, 256), (256, 512)), ((0, 256), (256, 512))]
+        pieces = [((0, 256), (256, 384), (384, 512)), ((0, 128), (128, 320), (320, 512)), ((0, 256), (256, 512))]
         x_raw = {
             (a, t0): keep.tile([P, 4, t1 - t0], F32, name=f"x_raw{a}_{t0}", tag=f"raw{a}_{t0}", align_bytes=64)
             for a in range(A)
@@ -41,8 +41,8 @@ def tile_moe_tk_lin_relu2_kernel(
         }
         x_bf = [reuse.tile([P, T, 4], BF16, name="x_bf0", align_bytes=64, offset=1024)]
         x_bf.extend(keep.tile([P, T, 4], BF16, name=f"x_bf{a}", tag=f"share{a}", align_bytes=64) for a in (1, 2))
-        all_codes = keep.tile([P, (A - 1) * T + 1376], I32, name="all_codes", align_bytes=64)
-        codes = [all_codes[:, (A - 1 - a) * T : (A - 1 - a) * T + 1376] for a in range(A)]
+        all_codes = keep.tile([P, (A - 1) * T + 2048], I32, name="all_codes", align_bytes=64)
+        codes = [all_codes[:, (A - 1 - a) * T : (A - 1 - a) * T + 2048] for a in range(A)]
         planes = keep.tile([P, 1376], U8, name="planes", tag="planes", align_bytes=64)
         slot_codes = {}
         gathered_planes = keep.tile([P, SLOTS], U8, name="gathered_planes", align_bytes=64)
@@ -93,7 +93,8 @@ def tile_moe_tk_lin_relu2_kernel(
                 )[:]
             for s in range(s0, s1, N):
                 slot_codes[(a, s)] = words[:, s - s0 : s - s0 + N]
-            width = 1376 if s1 - s0 > 512 else 704
+            width = -(-(s1 - s0) * 4 // 3 // 32) * 32 + 32 if s1 - s0 < 1536 else 2048
+            width = max(width, 704)
             nc.vector.tensor_copy(
                 words.bitcast(U32),
                 codes[a][:, 0:width].bitcast(U32).indirect(offs_t[:, s0 // 16 : s1 // 16]),
@@ -109,26 +110,34 @@ def tile_moe_tk_lin_relu2_kernel(
                     )
 
         acc = {}
+        bank_of = {}
 
-        def multiply(e, h, passes):
+        def multiply(e, h, a, opens, closes):
             cols = slice(e * C + h * N, e * C + h * N + N)
-            for a in passes:
-                nc.tensor.matmul_mx(
-                    out=acc[(e, h)],
-                    lhsT=w_t[:, e * A + a, :].bitcast(FP4X4),
-                    lhsT_scale=ws_t[:, e * A + a, :],
-                    rhs=slot_codes[(a, e * C + h * N)].bitcast(FP8X4),
-                    rhs_scale=slot_planes[a][:, cols],
-                    start=(a == 0),
-                    stop=(a == A - 1),
-                )
+            nc.tensor.matmul_mx(
+                out=acc[(e, h)],
+                lhsT=w_t[:, e * A + a, :].bitcast(FP4X4),
+                lhsT_scale=ws_t[:, e * A + a, :],
+                rhs=slot_codes[(a, e * C + h * N)].bitcast(FP8X4),
+                rhs_scale=slot_planes[a][:, cols],
+                start=opens,
+                stop=closes,
+            )
 
-        def open_bank(e):
-            tag = ("bank0", "bank1", "even", "odd", "even", "odd", "even")[e]
-            bank = psum.tile([P, 1024 if tag == "odd" else 512], F32, name=f"acc{e}", tag=tag)
-            for h in range(2):
-                acc[(e, h)] = bank[:, h * N : (h + 1) * N]
-            acc[e] = bank
+        groups = [((0, 0), (0, 1), (1, 0), (1, 1))]
+        groups.extend(((e, 0), (e, 1)) for e in range(2, 7))
+        groups.extend(((7, h),) for h in range(2))
+
+        def multiply_group(g, a, last=False):
+            for i, (e, h) in enumerate(groups[g]):
+                multiply(e, h, a, opens=(a == 0 and i == 0), closes=(last and i == len(groups[g]) - 1))
+
+        def open_bank(g):
+            bank = psum.tile([P, 512], F32, name=f"acc{g}", tag=f"bank{g}")
+            for i, (e, h) in enumerate(groups[g]):
+                acc[(e, h)] = bank[:, i * N : (i + 1) * N]
+                if h == 0:
+                    acc[e] = bank[:, i * N : (i + 2) * N]
 
         interleave(nc.vector.tensor_copy, 0, 0, 192)
         interleave(nc.scalar.copy, 0, 192, 256)
@@ -147,14 +156,13 @@ def tile_moe_tk_lin_relu2_kernel(
         moved_planes = reuse.tile([P, 2 * SLOTS], U8, name="moved_planes", align_bytes=64, offset=E * A * N)
         nc.gpsimd.memset(moved_planes[:].bitcast(I32), 0)
         slot_planes = [gathered_planes[:], moved_planes[:, 0:SLOTS], moved_planes[:, SLOTS : 2 * SLOTS]]
-        gather_words(0, 0, 1024)
+        gather_words(0, 0, 1536)
         for t0, t1 in pieces[1]:
             interleave(nc.scalar.copy, 1, t0, t1)
-        gather_words(0, 1024, 1920)
         quantise(1, 0, 512)
         ident = keep.tile([P, P], F32, name="ident", tag="share1", align_bytes=64)
         make_identity(nc, ident[:])
-        gather_words(0, 1920, 2048, tag="raw1_256")
+        gather_words(0, 1536, 2048, tag="raw1_320")
         for t0, t1 in pieces[2]:
             interleave(nc.scalar.copy, 2, t0, t1)
         gather_words(1, 0, 896)
@@ -164,60 +172,50 @@ def tile_moe_tk_lin_relu2_kernel(
         gather_bytes(1024, 2048)
         gate_t = keep.tile([P, TOP, T], F32, name="gate_t", tag="planes", align_bytes=64)
         nc.sync.dma_start(out=gate_t[:], in_=gate.rearrange("r p t -> p r t"))
-        for e in range(4):
-            open_bank(e)
-            multiply(e, 0, (0,))
-        for e in range(4):
-            multiply(e, 0, (1,))
-        rel_pair = [keep.tile([P, 2 * C], F32, name=f"rel_pair{i}") for i in range(3)]
-        for i in range(2):
-            gather_words(2, 512 * i, 512 * i + 512)
+        for g in range(len(groups)):
+            open_bank(g)
+            multiply_group(g, 0)
+        for g in range(3):
+            multiply_group(g, 1)
+
+        def finish_pair(i):
+            rel_pair = keep.tile([P, 2 * C], F32, name=f"rel_pair{i}", tag="rel")
             for e in (2 * i, 2 * i + 1):
-                multiply(e, 0, (2,))
-                multiply(e, 1, (0, 1, 2))
-        for e in range(4):
-            nc.scalar.activation(
-                rel_pair[e // 2][:, (e % 2) * C : (e % 2 + 1) * C], acc[e][:, 0:C], ACT.Relu, bias=b_t[:, e : e + 1]
-            )
-        for i in range(2):
-            nc.scalar.activation(y_t[:, 512 * i : 512 * i + 512], rel_pair[i][:], ACT.Square)
+                nc.scalar.activation(
+                    rel_pair[:, (e % 2) * C : (e % 2 + 1) * C], acc[e], ACT.Relu, bias=b_t[:, e : e + 1]
+                )
+            nc.scalar.activation(y_t[:, 512 * i : 512 * i + 512], rel_pair[:], ACT.Square)
+
+        gather_words(2, 0, 512)
+        multiply_group(0, 2, last=True)
+        finish_pair(0)
+        gather_words(2, 512, 1024)
+        for g in (1, 2):
+            multiply_group(g, 2, last=True)
+        finish_pair(1)
         late_words = keep.tile([P, 1024], I32, name="late_words", tag="share2", align_bytes=64)
         gather_words(1, 1024, 1536, words=late_words[:, 0:512])
-        for e in (4, 5):
-            open_bank(e)
-            multiply(e, 0, (0, 1))
+        for g in (3, 4):
+            multiply_group(g, 1)
         gather_words(2, 1024, 1536)
-        for e in (4, 5):
-            multiply(e, 0, (2,))
-            multiply(e, 1, (0, 1, 2))
-        for e in (4, 5):
-            nc.scalar.activation(
-                rel_pair[2][:, (e % 2) * C : (e % 2 + 1) * C], acc[e][:, 0:C], ACT.Relu, bias=b_t[:, e : e + 1]
-            )
-        nc.scalar.activation(y_t[:, 5 * C : 6 * C], rel_pair[2][:, C : 2 * C], ACT.Square)
+        for g in (3, 4):
+            multiply_group(g, 2, last=True)
+        finish_pair(2)
+        gather_words(2, 1536, 2048)
+        for g in (5, 6, 7):
+            multiply_group(g, 2)
         gather_words(1, 1536, 1792, words=late_words[:, 512:768])
-        open_bank(6)
-        multiply(6, 0, (0, 1))
-        gather_words(2, 1536, 1792)
-        multiply(6, 0, (2,))
-        multiply(6, 1, (0, 1, 2))
-        rel6 = keep.tile([P, C], F32, name="rel6")
-        nc.scalar.activation(rel6[:], acc[6][:, 0:C], ACT.Relu, bias=b_t[:, 6:7])
+        multiply_group(5, 1, last=True)
+        rel6 = keep.tile([P, C], F32, name="rel6", tag="rel")
+        nc.scalar.activation(rel6[:], acc[6], ACT.Relu, bias=b_t[:, 6:7])
         nc.scalar.activation(y_t[:, 6 * C : 7 * C], rel6[:], ACT.Square)
-        gather_words(1, 1792, 2048, words=late_words[:, 768:1024])
-        last_banks = psum.tile([P, 1024], F32, name="acc7", tag="odd")
-        for h in range(2):
-            acc[(7, h)] = last_banks[:, 512 * h : 512 * h + N]
-            multiply(7, h, (0, 1))
-        gather_words(2, 1792, 1920)
-        gather_words(2, 1920, 2048)
-        nc.vector.tensor_tensor(y_t[:, 4 * C : 5 * C], rel_pair[2][:, 0:C], rel_pair[2][:, 0:C], ALU.mult)
-        for h in range(2):
-            multiply(7, h, (2,))
+        gather_words(1, 1792, 1920, words=late_words[:, 768:896])
+        multiply_group(6, 1, last=True)
+        gather_words(1, 1920, 2048, words=late_words[:, 896:1024])
+        multiply_group(7, 1, last=True)
         rel7 = [keep.tile([P, N], F32, name=f"rel7_{h}") for h in range(2)]
         for h in range(2):
             nc.vector.tensor_scalar(rel7[h][:], acc[(7, h)], b_t[:, 7:8], 0.0, ALU.add, ALU.max)
-        for h in range(2):
             nc.vector.tensor_tensor(y_t[:, 7 * C + h * N : 7 * C + (h + 1) * N], rel7[h][:], rel7[h][:], ALU.mult)
 
         cut = 2 * P
@@ -232,8 +230,7 @@ def tile_moe_tk_lin_relu2_kernel(
             )
             return product
 
-        turned = [psum.tile([P, 512], F32, name=f"turned{blk}") for blk in range(3)]
-        turned.append(psum.tile([P, 512], F32, name="turned3", tag="bank0"))
+        turned = [psum.tile([P, 512], F32, name=f"turned{blk}", tag=f"bank{blk}") for blk in range(4)]
 
         def turn(product, blk, first, last):
             nc.tensor.matmul(
@@ -255,8 +252,8 @@ def tile_moe_tk_lin_relu2_kernel(
         product = fetch(2, 0, cut)
         for blk in range(2):
             turn(product, blk, False, True)
-        partial_b = turn_back((2, 3), "bank1")
-        partial_a = turn_back((0, 1), "even")
+        partial_b = turn_back((2, 3), "bank4")
+        partial_a = turn_back((0, 1), "bank5")
         third_b = fetch(2, cut, T)
         fourth = fetch(3, 0, T)
         sum_b = keep.tile([P, T - cut], F32, name="sum_b")

@@ -67,6 +67,11 @@ def tile_moe_tk_lin_relu2_kernel(
         for r, pos in enumerate((pos1, pos2, pos3, pos4)):
             nc.sync.dma_start(pos_t[r][:], pos)
 
+        gate_cols = [keep.tile([P, T // P], F32, name=f"gate_cols{r}") for r in (2, 3)]
+        with nc.allow_non_contiguous_dma(reason="one gate value a partition"):
+            for i, r in enumerate((2, 3)):
+                nc.sync.dma_start(out=gate_cols[i][:], in_=gate[r, 0, :].rearrange("(b p) -> p b", p=P))
+
         nc.vector.memset(warm[:, 0:1], 0.0)
         nc.scalar.activation(warm[:, 1:2], warm[:, 0:1], ACT.Relu)
         nc.vector.memset(planes[:].bitcast(I32), 0)
@@ -170,8 +175,8 @@ def tile_moe_tk_lin_relu2_kernel(
         gather_words(1, 896, 1024, tag="raw2_256")
         gather_bytes(0, 1024)
         gather_bytes(1024, 2048)
-        gate_t = keep.tile([P, TOP, T], F32, name="gate_t", tag="planes", align_bytes=64)
-        nc.sync.dma_start(out=gate_t[:], in_=gate.rearrange("r p t -> p r t"))
+        gate_t = keep.tile([P, 3, T], F32, name="gate_t", tag="planes", align_bytes=64)
+        nc.sync.dma_start(out=gate_t[:], in_=gate[0:3].rearrange("r p t -> p r t"))
         for g in range(len(groups)):
             open_bank(g)
             multiply_group(g, 0)
@@ -218,49 +223,52 @@ def tile_moe_tk_lin_relu2_kernel(
             nc.vector.tensor_scalar(rel7[h][:], acc[(7, h)], b_t[:, 7:8], 0.0, ALU.add, ALU.max)
             nc.vector.tensor_tensor(y_t[:, 7 * C + h * N : 7 * C + (h + 1) * N], rel7[h][:], rel7[h][:], ALU.mult)
 
-        cut = 2 * P
-
-        def fetch(r, t0, t1):
-            product = keep.tile([P, t1 - t0], F32, name=f"product{r}_{t0}")
-            nc.vector.tensor_tensor(
-                product[:],
-                y_t[:].indirect(pos_t[r][:, t0 // 16 : t1 // 16]),
-                gate_t[:, r, t0:t1],
-                ALU.mult,
-            )
-            return product
-
-        turned = [psum.tile([P, 512], F32, name=f"turned{blk}", tag=f"bank{blk}") for blk in range(4)]
-
-        def turn(product, blk, first, last):
-            nc.tensor.matmul(
-                turned[blk][:, 0:P], product[:, blk * P : (blk + 1) * P], ident[:], start=first, stop=last, is_transpose=True
-            )
-
-        def turn_back(blocks, tag):
-            partial = psum.tile([P, 512], F32, name=f"partial{blocks[0]}", tag=tag)
-            for i, blk in enumerate(blocks):
-                staged = keep.tile([P, P], F32, name=f"staged{blk}", tag=f"staged{blk}")
-                nc.scalar.copy(staged[:], turned[blk][:, 0:P])
-                nc.tensor.transpose(partial[:, i * P : (i + 1) * P], staged[:], ident[:])
-            return partial
-
-        for r in range(2):
-            product = fetch(r, 0, T)
-            for blk in (2, 3, 0, 1):
-                turn(product, blk, r == 0, r == 1 and blk >= 2)
-        product = fetch(2, 0, cut)
-        for blk in range(2):
-            turn(product, blk, False, True)
-        partial_b = turn_back((2, 3), "bank4")
-        partial_a = turn_back((0, 1), "bank5")
-        third_b = fetch(2, cut, T)
-        fourth = fetch(3, 0, T)
+        cut = T - 3 * P
+        blocks = T // P
+        first_shared = cut // P
+        span = {3: (0, T), 2: (cut, T)}
+        plain = {}
+        for r in (3, 2):
+            t0, t1 = span[r]
+            plain[r] = keep.tile([P, t1 - t0], F32, name=f"plain{r}")
+            nc.scalar.activation(plain[r][:], y_t[:].indirect(pos_t[r][:, t0 // 16 : t1 // 16]), ACT.Copy)
+        products = []
+        for r, t1 in ((0, T), (1, T), (2, cut)):
+            product = keep.tile([P, t1], F32, name=f"product{r}")
+            nc.vector.tensor_tensor(product[:], y_t[:].indirect(pos_t[r][:, 0 : t1 // 16]), gate_t[:, r, 0:t1], ALU.mult)
+            products.append(product)
+        turned = {}
+        for r in (3, 2):
+            t0, t1 = span[r]
+            turned[r] = psum.tile([P, 512], F32, name=f"turned{r}", tag=f"bank{r}")
+            for blk in range(t0 // P, blocks):
+                nc.tensor.transpose(
+                    turned[r][:, blk * P : (blk + 1) * P], plain[r][:, blk * P - t0 : (blk + 1) * P - t0], ident[:]
+                )
+        partial_a = psum.tile([P, 512], F32, name="partial_a", tag="bank0")
+        partial = {blk: partial_a[:, blk * P : (blk + 1) * P] for blk in range(first_shared)}
+        for blk in range(first_shared, blocks):
+            bank = psum.tile([P, 512], F32, name=f"partial{blk}", tag=f"bank{blk + 3}")
+            partial[blk] = bank[:, 0:P]
+        for r in (3, 2):
+            for blk in range(span[r][0] // P, blocks):
+                gated = keep.tile([P, P], F32, name=f"gated{r}_{blk}")
+                nc.scalar.activation(
+                    gated[:], turned[r][:, blk * P : (blk + 1) * P], ACT.Copy, scale=gate_cols[r - 2][:, blk : blk + 1]
+                )
+                nc.tensor.matmul(
+                    partial[blk], gated[:], ident[:], start=(r == 3), stop=(r == 2 or blk < first_shared), is_transpose=True
+                )
+        outer_a = keep.tile([P, cut], F32, name="outer_a")
+        nc.vector.tensor_tensor(outer_a[:], products[0][:, 0:cut], products[2][:], ALU.add)
         sum_b = keep.tile([P, T - cut], F32, name="sum_b")
-        nc.vector.tensor_tensor(sum_b[:], partial_b[:, 0 : T - cut], third_b[:], ALU.add)
+        nc.vector.tensor_tensor(sum_b[:], products[0][:, cut:T], products[1][:, cut:T], ALU.add)
+        sum_a = keep.tile([P, cut], F32, name="sum_a")
+        nc.vector.tensor_tensor(sum_a[:], outer_a[:], products[1][:, 0:cut], ALU.add)
         result_a = keep.tile([P, cut], F32, name="result_a")
-        nc.vector.tensor_tensor(result_a[:], partial_a[:, 0:cut], fourth[:, 0:cut], ALU.add)
+        nc.vector.tensor_tensor(result_a[:], partial_a[:, 0:cut], sum_a[:], ALU.add)
         nc.sync.dma_start(out=out[:, 0:cut], in_=result_a[:])
-        result_b = keep.tile([P, T - cut], F32, name="result_b", tag="staged1")
-        nc.vector.tensor_tensor(result_b[:], sum_b[:], fourth[:, cut:T], ALU.add)
-        nc.sync.dma_start(out=out[:, cut:T], in_=result_b[:])
+        for blk in range(first_shared, blocks):
+            result = keep.tile([P, P], F32, name=f"result{blk}")
+            nc.vector.tensor_tensor(result[:], partial[blk], sum_b[:, blk * P - cut : (blk + 1) * P - cut], ALU.add)
+            nc.sync.dma_start(out=out[:, blk * P : (blk + 1) * P], in_=result[:])

@@ -67,11 +67,6 @@ def tile_moe_tk_lin_relu2_kernel(
         for r, pos in enumerate((pos1, pos2, pos3, pos4)):
             nc.sync.dma_start(pos_t[r][:], pos)
 
-        gate_cols = [keep.tile([P, T // P], F32, name=f"gate_cols{r}") for r in (2, 3)]
-        with nc.allow_non_contiguous_dma(reason="one gate value a partition"):
-            for i, r in enumerate((2, 3)):
-                nc.sync.dma_start(out=gate_cols[i][:], in_=gate[r, 0, :].rearrange("(b p) -> p b", p=P))
-
         nc.vector.memset(warm[:, 0:1], 0.0)
         nc.scalar.activation(warm[:, 1:2], warm[:, 0:1], ACT.Relu)
         nc.vector.memset(planes[:].bitcast(I32), 0)
@@ -175,8 +170,22 @@ def tile_moe_tk_lin_relu2_kernel(
         gather_words(1, 896, 1024, tag="raw2_256")
         gather_bytes(0, 1024)
         gather_bytes(1024, 2048)
-        gate_t = keep.tile([P, 3, T], F32, name="gate_t", tag="planes", align_bytes=64)
-        nc.sync.dma_start(out=gate_t[:], in_=gate[0:3].rearrange("r p t -> p r t"))
+        cut = P
+        blocks = T // P
+        gates = keep.tile([P, 2 * T + cut + 16], F32, name="gates", tag="planes", align_bytes=64)
+        gate_rows = [gates[:, 0:T], gates[:, T : 2 * T], gates[:, 2 * T : 2 * T + cut]]
+        gate_cols = {r: gates[:, 2 * T + cut + 8 * (r - 2) : 2 * T + cut + 8 * (r - 2) + blocks] for r in (2, 3)}
+        span = {3: (0, T), 2: (cut, T)}
+        nc.sync.dma_start(
+            out=gates[:, 0 : 2 * T].rearrange("p (r t) -> p r t", r=2), in_=gate[0:2].rearrange("r p t -> p r t")
+        )
+        nc.sync.dma_start(out=gate_rows[2], in_=gate[2, :, 0:cut])
+        with nc.allow_non_contiguous_dma(reason="one gate value a partition"):
+            for r in (3, 2):
+                t0 = span[r][0]
+                nc.sync.dma_start(
+                    out=gate_cols[r][:, t0 // P : blocks], in_=gate[r, 0, t0:T].rearrange("(b p) -> p b", p=P)
+                )
         for g in range(len(groups)):
             open_bank(g)
             multiply_group(g, 0)
@@ -221,54 +230,53 @@ def tile_moe_tk_lin_relu2_kernel(
         rel7 = [keep.tile([P, N], F32, name=f"rel7_{h}") for h in range(2)]
         for h in range(2):
             nc.vector.tensor_scalar(rel7[h][:], acc[(7, h)], b_t[:, 7:8], 0.0, ALU.add, ALU.max)
+        for h in range(2):
             nc.vector.tensor_tensor(y_t[:, 7 * C + h * N : 7 * C + (h + 1) * N], rel7[h][:], rel7[h][:], ALU.mult)
 
-        cut = T - 3 * P
-        blocks = T // P
-        first_shared = cut // P
-        span = {3: (0, T), 2: (cut, T)}
         plain = {}
         for r in (3, 2):
             t0, t1 = span[r]
             plain[r] = keep.tile([P, t1 - t0], F32, name=f"plain{r}")
             nc.scalar.activation(plain[r][:], y_t[:].indirect(pos_t[r][:, t0 // 16 : t1 // 16]), ACT.Copy)
-        products = []
-        for r, t1 in ((0, T), (1, T), (2, cut)):
-            product = keep.tile([P, t1], F32, name=f"product{r}")
-            nc.vector.tensor_tensor(product[:], y_t[:].indirect(pos_t[r][:, 0 : t1 // 16]), gate_t[:, r, 0:t1], ALU.mult)
-            products.append(product)
+        products = {}
+        for r, t1 in ((0, T), (2, cut), (1, T)):
+            products[r] = keep.tile([P, t1], F32, name=f"product{r}")
+            nc.vector.tensor_tensor(
+                products[r][:], y_t[:].indirect(pos_t[r][:, 0 : t1 // 16]), gate_rows[r], ALU.mult
+            )
         turned = {}
+        fourth_bank = psum.tile([P, 512], F32, name="turned3", tag="bank0")
+        for blk in range(blocks):
+            turned[(3, blk)] = fourth_bank[:, blk * P : (blk + 1) * P]
+        for blk in range(cut // P, blocks):
+            bank = psum.tile([P, 512], F32, name=f"turned2_{blk}", tag=f"bank{blk}")
+            turned[(2, blk)] = bank[:, 0:P]
         for r in (3, 2):
-            t0, t1 = span[r]
-            turned[r] = psum.tile([P, 512], F32, name=f"turned{r}", tag=f"bank{r}")
+            t0 = span[r][0]
             for blk in range(t0 // P, blocks):
-                nc.tensor.transpose(
-                    turned[r][:, blk * P : (blk + 1) * P], plain[r][:, blk * P - t0 : (blk + 1) * P - t0], ident[:]
-                )
-        partial_a = psum.tile([P, 512], F32, name="partial_a", tag="bank0")
-        partial = {blk: partial_a[:, blk * P : (blk + 1) * P] for blk in range(first_shared)}
-        for blk in range(first_shared, blocks):
-            bank = psum.tile([P, 512], F32, name=f"partial{blk}", tag=f"bank{blk + 3}")
+                nc.tensor.transpose(turned[(r, blk)], plain[r][:, blk * P - t0 : (blk + 1) * P - t0], ident[:])
+        partial = {}
+        for blk in range(blocks):
+            bank = psum.tile([P, 512], F32, name=f"partial{blk}", tag=f"bank{blk + 4}")
             partial[blk] = bank[:, 0:P]
         for r in (3, 2):
             for blk in range(span[r][0] // P, blocks):
                 gated = keep.tile([P, P], F32, name=f"gated{r}_{blk}")
-                nc.scalar.activation(
-                    gated[:], turned[r][:, blk * P : (blk + 1) * P], ACT.Copy, scale=gate_cols[r - 2][:, blk : blk + 1]
-                )
+                nc.scalar.activation(gated[:], turned[(r, blk)], ACT.Copy, scale=gate_cols[r][:, blk : blk + 1])
                 nc.tensor.matmul(
-                    partial[blk], gated[:], ident[:], start=(r == 3), stop=(r == 2 or blk < first_shared), is_transpose=True
+                    partial[blk], gated[:], ident[:], start=(r == 3), stop=(r == 2 or blk < cut // P), is_transpose=True
                 )
-        outer_a = keep.tile([P, cut], F32, name="outer_a")
-        nc.vector.tensor_tensor(outer_a[:], products[0][:, 0:cut], products[2][:], ALU.add)
-        sum_b = keep.tile([P, T - cut], F32, name="sum_b")
-        nc.vector.tensor_tensor(sum_b[:], products[0][:, cut:T], products[1][:, cut:T], ALU.add)
-        sum_a = keep.tile([P, cut], F32, name="sum_a")
-        nc.vector.tensor_tensor(sum_a[:], outer_a[:], products[1][:, 0:cut], ALU.add)
-        result_a = keep.tile([P, cut], F32, name="result_a")
-        nc.vector.tensor_tensor(result_a[:], partial_a[:, 0:cut], sum_a[:], ALU.add)
-        nc.sync.dma_start(out=out[:, 0:cut], in_=result_a[:])
-        for blk in range(first_shared, blocks):
-            result = keep.tile([P, P], F32, name=f"result{blk}")
-            nc.vector.tensor_tensor(result[:], partial[blk], sum_b[:, blk * P - cut : (blk + 1) * P - cut], ALU.add)
+
+        def add(name, t0, t1, left, right):
+            total = keep.tile([P, t1 - t0], F32, name=name)
+            nc.vector.tensor_tensor(total[:], left, right, ALU.add)
+            return total
+
+        outer = add("outer", 0, cut, products[0][:, 0:cut], products[2][:])
+        sum_1 = add("sum_1", P, 2 * P, products[0][:, P : 2 * P], products[1][:, P : 2 * P])
+        sum_0 = add("sum_0", 0, P, outer[:], products[1][:, 0:P])
+        sum_23 = add("sum_23", 2 * P, T, products[0][:, 2 * P : T], products[1][:, 2 * P : T])
+        sums = [sum_0[:], sum_1[:], sum_23[:, 0:P], sum_23[:, P : 2 * P]]
+        for blk in range(blocks):
+            result = add(f"result{blk}", 0, P, partial[blk], sums[blk])
             nc.sync.dma_start(out=out[:, blk * P : (blk + 1) * P], in_=result[:])

@@ -8,6 +8,7 @@ TOP = 4
 SLOTS = E * C
 P = 128
 A = K // 512
+HALF = T // 2
 FLOPS = 2 * K * N * SLOTS
 
 F32 = mybir.dt.float32
@@ -33,12 +34,7 @@ def tile_moe_tk_lin_relu2_kernel(
 
         offs_t = keep.tile([P, SLOTS // 16], U16, name="offs_t")
         pos_t = [keep.tile([P, T // 16], U16, name=f"pos_t{r}") for r in range(TOP)]
-        pieces = [((0, 256), (256, 384), (384, 512)), ((0, 128), (128, 320), (320, 512)), ((0, 256), (256, 512))]
-        x_raw = {
-            (a, t0): keep.tile([P, 4, t1 - t0], F32, name=f"x_raw{a}_{t0}", tag=f"raw{a}_{t0}", align_bytes=64)
-            for a in range(A)
-            for t0, t1 in pieces[a]
-        }
+        x_raw = [keep.tile([P, 4, T], F32, name=f"x_raw{a}", tag=f"raw{a}", align_bytes=64) for a in range(A)]
         x_bf = [reuse.tile([P, T, 4], BF16, name="x_bf0", align_bytes=64, offset=1024)]
         x_bf.extend(keep.tile([P, T, 4], BF16, name=f"x_bf{a}", tag=f"share{a}", align_bytes=64) for a in (1, 2))
         all_codes = keep.tile([P, (A - 1) * T + 2048], I32, name="all_codes", align_bytes=64)
@@ -51,12 +47,11 @@ def tile_moe_tk_lin_relu2_kernel(
         y_t = keep.tile([P, SLOTS], F32, name="y_t")
         warm = keep.tile([P, 2], F32, name="warm")
 
-        def x_rows(a):
-            return xT[a * 512 : (a + 1) * 512, :].rearrange("(p j) t -> p j t", j=4)
-
         for a in range(A):
-            for t0, t1 in pieces[a]:
-                nc.sync.dma_start(out=x_raw[(a, t0)][:], in_=x_rows(a)[:, :, t0:t1])
+            rows = xT[a * 512 : (a + 1) * 512, :].rearrange("(p j) t -> p j t", j=4)
+            nc.sync.dma_start(out=x_raw[a][:, 0:2, :], in_=rows[:, 0:2, :])
+            for t0 in (0, HALF):
+                nc.sync.dma_start(out=x_raw[a][:, 2:4, t0 : t0 + HALF], in_=rows[:, 2:4, t0 : t0 + HALF])
             if a == 0:
                 nc.sync.dma_start(offs_t[:], offs)
 
@@ -73,10 +68,9 @@ def tile_moe_tk_lin_relu2_kernel(
         nc.vector.memset(all_codes[:, A * T :], 0)
 
         def interleave(copy, a, t0, t1):
-            base = max(p0 for p0, p1 in pieces[a] if p0 <= t0)
             copy(
                 x_bf[a][:, t0:t1, :].rearrange("p (c i) j -> p c j i", i=4),
-                x_raw[(a, base)][:, :, t0 - base : t1 - base].rearrange("p j (c i) -> p c j i", i=4),
+                x_raw[a][:, :, t0:t1].rearrange("p j (c i) -> p c j i", i=4),
             )
 
         def quantise(a, t0, t1):
@@ -93,8 +87,7 @@ def tile_moe_tk_lin_relu2_kernel(
                 )[:]
             for s in range(s0, s1, N):
                 slot_codes[(a, s)] = words[:, s - s0 : s - s0 + N]
-            width = -(-(s1 - s0) * 4 // 3 // 32) * 32 + 32 if s1 - s0 < 1536 else 2048
-            width = max(width, 704)
+            width = max(704, -(-(s1 - s0) * 4 // 3 // 32) * 32)
             nc.vector.tensor_copy(
                 words.bitcast(U32),
                 codes[a][:, 0:width].bitcast(U32).indirect(offs_t[:, s0 // 16 : s1 // 16]),
@@ -110,7 +103,6 @@ def tile_moe_tk_lin_relu2_kernel(
                     )
 
         acc = {}
-        bank_of = {}
 
         def multiply(e, h, a, opens, closes):
             cols = slice(e * C + h * N, e * C + h * N + N)
@@ -139,11 +131,11 @@ def tile_moe_tk_lin_relu2_kernel(
                 if h == 0:
                     acc[e] = bank[:, i * N : (i + 2) * N]
 
-        interleave(nc.vector.tensor_copy, 0, 0, 192)
-        interleave(nc.scalar.copy, 0, 192, 256)
+        interleave(nc.vector.tensor_copy, 0, 0, 160)
+        interleave(nc.scalar.copy, 0, 160, 256)
         quantise(0, 0, 256)
-        interleave(nc.scalar.copy, 0, 256, 384)
-        interleave(nc.vector.tensor_copy, 0, 384, 512)
+        interleave(nc.vector.tensor_copy, 0, 256, 384)
+        interleave(nc.scalar.copy, 0, 384, 512)
         quantise(0, 256, 384)
         quantise(0, 384, 512)
         ws_t = reuse.tile([P, E * A, N], U8, name="ws_t", align_bytes=64, offset=0)
@@ -157,17 +149,17 @@ def tile_moe_tk_lin_relu2_kernel(
         nc.gpsimd.memset(moved_planes[:].bitcast(I32), 0)
         slot_planes = [gathered_planes[:], moved_planes[:, 0:SLOTS], moved_planes[:, SLOTS : 2 * SLOTS]]
         gather_words(0, 0, 1536)
-        for t0, t1 in pieces[1]:
-            interleave(nc.scalar.copy, 1, t0, t1)
+        for t0 in (0, HALF):
+            interleave(nc.scalar.copy, 1, t0, t0 + HALF)
         quantise(1, 0, 512)
         ident = keep.tile([P, P], F32, name="ident", tag="share1", align_bytes=64)
         make_identity(nc, ident[:])
-        gather_words(0, 1536, 2048, tag="raw1_320")
-        for t0, t1 in pieces[2]:
-            interleave(nc.scalar.copy, 2, t0, t1)
-        gather_words(1, 0, 896)
+        gather_words(0, 1536, 2048, tag="raw1")
+        for t0 in (0, HALF):
+            interleave(nc.scalar.copy, 2, t0, t0 + HALF)
+        gather_words(1, 0, 512)
         quantise(2, 0, 512)
-        gather_words(1, 896, 1024, tag="raw2_256")
+        gather_words(1, 512, 640, tag="raw2")
         gather_bytes(0, 1024)
         gather_bytes(1024, 2048)
         cut = P
@@ -189,8 +181,6 @@ def tile_moe_tk_lin_relu2_kernel(
         for g in range(len(groups)):
             open_bank(g)
             multiply_group(g, 0)
-        for g in range(3):
-            multiply_group(g, 1)
 
         def finish_pair(i):
             rel_pair = keep.tile([P, 2 * C], F32, name=f"rel_pair{i}", tag="rel")
@@ -200,15 +190,17 @@ def tile_moe_tk_lin_relu2_kernel(
                 )
             nc.scalar.activation(y_t[:, 512 * i : 512 * i + 512], rel_pair[:], ACT.Square)
 
-        gather_words(2, 0, 512)
+        late_words = keep.tile([P, 1408], I32, name="late_words", tag="share2", align_bytes=64)
+        multiply_group(0, 1)
+        gather_words(2, 0, 1024)
         multiply_group(0, 2, last=True)
         finish_pair(0)
-        gather_words(2, 512, 1024)
         for g in (1, 2):
-            multiply_group(g, 2, last=True)
+            multiply_group(g, 2)
+        gather_words(1, 640, 1536, words=late_words[:, 0:896])
+        for g in (1, 2):
+            multiply_group(g, 1, last=True)
         finish_pair(1)
-        late_words = keep.tile([P, 1024], I32, name="late_words", tag="share2", align_bytes=64)
-        gather_words(1, 1024, 1536, words=late_words[:, 0:512])
         for g in (3, 4):
             multiply_group(g, 1)
         gather_words(2, 1024, 1536)
@@ -218,14 +210,14 @@ def tile_moe_tk_lin_relu2_kernel(
         gather_words(2, 1536, 2048)
         for g in (5, 6, 7):
             multiply_group(g, 2)
-        gather_words(1, 1536, 1792, words=late_words[:, 512:768])
+        gather_words(1, 1536, 1792, words=late_words[:, 896:1152])
         multiply_group(5, 1, last=True)
         rel6 = keep.tile([P, C], F32, name="rel6", tag="rel")
         nc.scalar.activation(rel6[:], acc[6], ACT.Relu, bias=b_t[:, 6:7])
         nc.scalar.activation(y_t[:, 6 * C : 7 * C], rel6[:], ACT.Square)
-        gather_words(1, 1792, 1920, words=late_words[:, 768:896])
+        gather_words(1, 1792, 1920, words=late_words[:, 1152:1280])
         multiply_group(6, 1, last=True)
-        gather_words(1, 1920, 2048, words=late_words[:, 896:1024])
+        gather_words(1, 1920, 2048, words=late_words[:, 1280:1408])
         multiply_group(7, 1, last=True)
         rel7 = [keep.tile([P, N], F32, name=f"rel7_{h}") for h in range(2)]
         for h in range(2):

@@ -37,8 +37,8 @@ def tile_moe_tk_lin_relu2_kernel(
         x_raw = [keep.tile([P, 4, T], F32, name=f"x_raw{a}", tag=f"raw{a}", align_bytes=64) for a in range(A)]
         x_bf = [reuse.tile([P, T, 4], BF16, name="x_bf0", align_bytes=64, offset=1024)]
         x_bf.extend(keep.tile([P, T, 4], BF16, name=f"x_bf{a}", tag=f"share{a}", align_bytes=64) for a in (1, 2))
-        all_codes = keep.tile([P, (A - 1) * T + 2048], I32, name="all_codes", align_bytes=64)
-        codes = [all_codes[:, (A - 1 - a) * T : (A - 1 - a) * T + 2048] for a in range(A)]
+        all_codes = keep.tile([P, (A - 1) * T + 3584], I32, name="all_codes", align_bytes=64)
+        codes = [all_codes[:, (A - 1 - a) * T : (A - 1 - a) * T + 3584] for a in range(A)]
         planes = keep.tile([P, 1376], U8, name="planes", tag="planes", align_bytes=64)
         slot_codes = {}
         gathered_planes = keep.tile([P, SLOTS], U8, name="gathered_planes", align_bytes=64)
@@ -87,7 +87,7 @@ def tile_moe_tk_lin_relu2_kernel(
                 )[:]
             for s in range(s0, s1, N):
                 slot_codes[(a, s)] = words[:, s - s0 : s - s0 + N]
-            width = max(704, -(-(s1 - s0) * 4 // 3 // 32) * 32)
+            width = max(704, -(-(s1 - s0) * 4 // 3 // 32) * 32) if s1 - s0 <= 1536 else 2 * (s1 - s0)
             nc.vector.tensor_copy(
                 words.bitcast(U32),
                 codes[a][:, 0:width].bitcast(U32).indirect(offs_t[:, s0 // 16 : s1 // 16]),
@@ -148,13 +148,13 @@ def tile_moe_tk_lin_relu2_kernel(
         moved_planes = reuse.tile([P, 2 * SLOTS], U8, name="moved_planes", align_bytes=64, offset=E * A * N)
         nc.gpsimd.memset(moved_planes[:].bitcast(I32), 0)
         slot_planes = [gathered_planes[:], moved_planes[:, 0:SLOTS], moved_planes[:, SLOTS : 2 * SLOTS]]
-        gather_words(0, 0, 1536)
+        gather_words(0, 0, 1792)
         for t0 in (0, HALF):
             interleave(nc.scalar.copy, 1, t0, t0 + HALF)
         quantise(1, 0, 512)
         ident = keep.tile([P, P], F32, name="ident", tag="share1", align_bytes=64)
         make_identity(nc, ident[:])
-        gather_words(0, 1536, 2048, tag="raw1")
+        gather_words(0, 1792, 2048, tag="raw1")
         for t0 in (0, HALF):
             interleave(nc.scalar.copy, 2, t0, t0 + HALF)
         gather_words(1, 0, 512)
@@ -229,7 +229,10 @@ def tile_moe_tk_lin_relu2_kernel(
         for r in (3, 2):
             t0, t1 = span[r]
             plain[r] = keep.tile([P, t1 - t0], F32, name=f"plain{r}")
-            nc.scalar.activation(plain[r][:], y_t[:].indirect(pos_t[r][:, t0 // 16 : t1 // 16]), ACT.Copy)
+            for u0, u1 in ((t0, t1),) if r == 3 else ((t0, t1 - P), (t1 - P, t1)):
+                nc.scalar.activation(
+                    plain[r][:, u0 - t0 : u1 - t0], y_t[:].indirect(pos_t[r][:, u0 // 16 : u1 // 16]), ACT.Copy
+                )
         products = {}
         for r, t1 in ((0, T), (2, cut), (1, T)):
             products[r] = keep.tile([P, t1], F32, name=f"product{r}")

@@ -162,22 +162,16 @@ def tile_moe_tk_lin_relu2_kernel(
         gather_words(1, 512, 640, tag="raw2")
         gather_bytes(0, 1024)
         gather_bytes(1024, 2048)
-        cut = P
-        blocks = T // P
-        gates = keep.tile([P, 2 * T + cut + 16], F32, name="gates", tag="planes", align_bytes=64)
-        gate_rows = [gates[:, 0:T], gates[:, T : 2 * T], gates[:, 2 * T : 2 * T + cut]]
-        gate_cols = {r: gates[:, 2 * T + cut + 8 * (r - 2) : 2 * T + cut + 8 * (r - 2) + blocks] for r in (2, 3)}
-        span = {3: (0, T), 2: (cut, T)}
+        gates = keep.tile([P, TOP * 3 * P + 16], F32, name="gates", tag="planes", align_bytes=64)
+        gate_rows = gates[:, 0 : TOP * 3 * P].rearrange("p (r t) -> p r t", r=TOP)
+        gate_cols = gates[:, TOP * 3 * P :].rearrange("p (b r) -> p b r", b=2)
+        nc.sync.dma_start(out=gate_rows[:, 0:2, :], in_=gate[0:2, :, 0 : 3 * P].rearrange("r p t -> p r t"))
         nc.sync.dma_start(
-            out=gates[:, 0 : 2 * T].rearrange("p (r t) -> p r t", r=2), in_=gate[0:2].rearrange("r p t -> p r t")
+            out=gate_rows[:, 2:TOP, 0 : 2 * P], in_=gate[2:TOP, :, 0 : 2 * P].rearrange("r p t -> p r t")
         )
-        nc.sync.dma_start(out=gate_rows[2], in_=gate[2, :, 0:cut])
         with nc.allow_non_contiguous_dma(reason="one gate value a partition"):
-            for r in (3, 2):
-                t0 = span[r][0]
-                nc.sync.dma_start(
-                    out=gate_cols[r][:, t0 // P : blocks], in_=gate[r, 0, t0:T].rearrange("(b p) -> p b", p=P)
-                )
+            nc.sync.dma_start(out=gate_cols[:, 1, 0:TOP], in_=gate[:, 0, 3 * P : T].rearrange("r p -> p r"))
+            nc.sync.dma_start(out=gate_cols[:, 0, 2:TOP], in_=gate[2:TOP, 0, 2 * P : 3 * P].rearrange("r p -> p r"))
         for g in range(len(groups)):
             open_bank(g)
             multiply_group(g, 0)
@@ -225,53 +219,60 @@ def tile_moe_tk_lin_relu2_kernel(
         for h in range(2):
             nc.vector.tensor_tensor(y_t[:, 7 * C + h * N : 7 * C + (h + 1) * N], rel7[h][:], rel7[h][:], ALU.mult)
 
+        own, mixed = 2 * P, 3 * P
+        shared = 2
         plain = {}
-        for r in (3, 2):
-            t0, t1 = span[r]
-            plain[r] = keep.tile([P, t1 - t0], F32, name=f"plain{r}")
-            for u0, u1 in ((t0, t1),) if r == 3 else ((t0, t1 - P), (t1 - P, t1)):
-                nc.scalar.activation(
-                    plain[r][:, u0 - t0 : u1 - t0], y_t[:].indirect(pos_t[r][:, u0 // 16 : u1 // 16]), ACT.Copy
-                )
+        scalar_order = list(range(shared, TOP)) + list(range(shared))
+        for r in scalar_order:
+            t0 = mixed if r < shared else own
+            plain[r] = keep.tile([P, T - t0], F32, name=f"plain{r}")
+            nc.scalar.activation(plain[r][:], y_t[:].indirect(pos_t[r][:, t0 // 16 : T // 16]), ACT.Copy)
         products = {}
-        for r, t1 in ((0, T), (2, cut), (1, T)):
+
+        def fetch(r):
+            t1 = mixed if r < shared else own
             products[r] = keep.tile([P, t1], F32, name=f"product{r}")
             nc.vector.tensor_tensor(
-                products[r][:], y_t[:].indirect(pos_t[r][:, 0 : t1 // 16]), gate_rows[r], ALU.mult
+                products[r][:], y_t[:].indirect(pos_t[r][:, 0 : t1 // 16]), gate_rows[:, r, 0:t1], ALU.mult
             )
-        turned = {}
-        fourth_bank = psum.tile([P, 512], F32, name="turned3", tag="bank0")
-        for blk in range(blocks):
-            turned[(3, blk)] = fourth_bank[:, blk * P : (blk + 1) * P]
-        for blk in range(cut // P, blocks):
-            bank = psum.tile([P, 512], F32, name=f"turned2_{blk}", tag=f"bank{blk}")
-            turned[(2, blk)] = bank[:, 0:P]
-        for r in (3, 2):
-            t0 = span[r][0]
-            for blk in range(t0 // P, blocks):
-                nc.tensor.transpose(turned[(r, blk)], plain[r][:, blk * P - t0 : (blk + 1) * P - t0], ident[:])
-        partial = {}
-        for blk in range(blocks):
-            bank = psum.tile([P, 512], F32, name=f"partial{blk}", tag=f"bank{blk + 4}")
-            partial[blk] = bank[:, 0:P]
-        for r in (3, 2):
-            for blk in range(span[r][0] // P, blocks):
-                gated = keep.tile([P, P], F32, name=f"gated{r}_{blk}")
-                nc.scalar.activation(gated[:], turned[(r, blk)], ACT.Copy, scale=gate_cols[r][:, blk : blk + 1])
-                nc.tensor.matmul(
-                    partial[blk], gated[:], ident[:], start=(r == 3), stop=(r == 2 or blk < cut // P), is_transpose=True
-                )
 
-        def add(name, t0, t1, left, right):
-            total = keep.tile([P, t1 - t0], F32, name=name)
+        def add(name, width, left, right):
+            total = keep.tile([P, width], F32, name=name)
             nc.vector.tensor_tensor(total[:], left, right, ALU.add)
             return total
 
-        outer = add("outer", 0, cut, products[0][:, 0:cut], products[2][:])
-        sum_1 = add("sum_1", P, 2 * P, products[0][:, P : 2 * P], products[1][:, P : 2 * P])
-        sum_0 = add("sum_0", 0, P, outer[:], products[1][:, 0:P])
-        sum_23 = add("sum_23", 2 * P, T, products[0][:, 2 * P : T], products[1][:, 2 * P : T])
-        sums = [sum_0[:], sum_1[:], sum_23[:, 0:P], sum_23[:, P : 2 * P]]
-        for blk in range(blocks):
-            result = add(f"result{blk}", 0, P, partial[blk], sums[blk])
-            nc.sync.dma_start(out=out[:, blk * P : (blk + 1) * P], in_=result[:])
+        units = [(r, blk) for r in scalar_order for blk in ((3,) if r < shared else (2, 3))]
+        turned = {}
+        for i, (r, blk) in enumerate(units):
+            bank = psum.tile([P, 512], F32, name=f"turned{r}_{blk}", tag=f"bank{i % 6}")
+            turned[(r, blk)] = bank[:, 0:P]
+            t0 = mixed if r < shared else own
+            nc.tensor.transpose(turned[(r, blk)], plain[r][:, blk * P - t0 : (blk + 1) * P - t0], ident[:])
+        partial = {}
+        for blk in (2, 3):
+            bank = psum.tile([P, 512], F32, name=f"partial{blk}", tag=f"bank{blk + 4}")
+            partial[blk] = bank[:, 0:P]
+        for r, blk in units:
+            lists = [u for u, v in units if v == blk]
+            gated = keep.tile([P, P], F32, name=f"gated{r}_{blk}")
+            nc.scalar.activation(gated[:], turned[(r, blk)], ACT.Copy, scale=gate_cols[:, blk - 2, r : r + 1])
+            nc.tensor.matmul(
+                partial[blk], gated[:], ident[:], start=(r == lists[0]), stop=(r == lists[-1]), is_transpose=True
+            )
+        last_block = keep.tile([P, P], F32, name="last_block")
+        nc.scalar.copy(last_block[:], partial[3])
+        nc.sync.dma_start(out=out[:, mixed:T], in_=last_block[:])
+
+        fetch(0)
+        fetch(1)
+        fetch(2)
+        first = add("first", mixed, products[0][:], products[1][:])
+        fetch(3)
+        second = [
+            add(f"second{h}", P, first[:, h * P : (h + 1) * P], products[2][:, h * P : (h + 1) * P]) for h in range(2)
+        ]
+        third_block = add("third_block", P, partial[2], first[:, own:mixed])
+        nc.sync.dma_start(out=out[:, own:mixed], in_=third_block[:])
+        for h in range(2):
+            result = add(f"result{h}", P, second[h][:], products[3][:, h * P : (h + 1) * P])
+            nc.sync.dma_start(out=out[:, h * P : (h + 1) * P], in_=result[:])

@@ -68,9 +68,10 @@ def tile_moe_tk_lin_relu2_kernel(
         nc.vector.memset(all_codes[:, A * T :], 0)
 
         def interleave(copy, a, t0, t1):
+            run = 4 if t0 < HALF else 2
             copy(
-                x_bf[a][:, t0:t1, :].rearrange("p (c i) j -> p c j i", i=4),
-                x_raw[a][:, :, t0:t1].rearrange("p j (c i) -> p c j i", i=4),
+                x_bf[a][:, t0:t1, :].rearrange("p (c i) j -> p c j i", i=run),
+                x_raw[a][:, :, t0:t1].rearrange("p j (c i) -> p c j i", i=run),
             )
 
         def quantise(a, t0, t1):

from contextlib import ExitStack

import concourse.mybir as mybir
from concourse.masks import make_identity

K, T, E, C, N = 1536, 512, 8, 256, 128
TOP = 4
SLOTS = E * C
P = 128
A = K // 512
HALF = T // 2
FLOPS = 2 * K * N * SLOTS

F32 = mybir.dt.float32
BF16 = mybir.dt.bfloat16
I32 = mybir.dt.int32
U32 = mybir.dt.uint32
U16 = mybir.dt.uint16
U8 = mybir.dt.uint8
FP8X4 = mybir.dt.float8_e4m3fn_x4
FP4X4 = mybir.dt.float4_e2m1fn_x4
ACT = mybir.ActivationFunctionType
ALU = mybir.AluOpType


def tile_moe_tk_lin_relu2_kernel(
    tc, xT, w_words, w_scales, b, gate, offs, pos1, pos2, pos3, pos4, out
):
    nc = tc.nc
    with ExitStack() as ctx:
        keep = ctx.enter_context(tc.tile_pool(name="keep", bufs=1))
        reuse = ctx.enter_context(tc.tile_pool(name="reuse", bufs=1))
        psum = ctx.enter_context(tc.psum_pool(name="psum", bufs=1))

        offs_t = keep.tile([P, SLOTS // 16], U16, name="offs_t")
        pos_t = [keep.tile([P, T // 16], U16, name=f"pos_t{r}") for r in range(TOP)]
        x_raw = [keep.tile([P, 4, T], F32, name=f"x_raw{a}", tag=f"raw{a}", align_bytes=64) for a in range(A)]
        x_bf = [reuse.tile([P, T, 4], BF16, name="x_bf0", align_bytes=64, offset=1024)]
        x_bf.extend(keep.tile([P, T, 4], BF16, name=f"x_bf{a}", tag=f"share{a}", align_bytes=64) for a in (1, 2))
        all_codes = keep.tile([P, (A - 1) * T + 3584], I32, name="all_codes", align_bytes=64)
        codes = [all_codes[:, (A - 1 - a) * T : (A - 1 - a) * T + 3584] for a in range(A)]
        planes = keep.tile([P, 1376], U8, name="planes", tag="planes", align_bytes=64)
        slot_codes = {}
        gathered_planes = keep.tile([P, SLOTS], U8, name="gathered_planes", align_bytes=64)
        w_t = keep.tile([P, E * A, 2 * N], U8, name="w_t", align_bytes=64)
        b_t = keep.tile([P, E], F32, name="b_t")
        y_t = keep.tile([P, SLOTS], F32, name="y_t")
        warm = keep.tile([P, 2], F32, name="warm")

        for a in range(A):
            rows = xT[a * 512 : (a + 1) * 512, :].rearrange("(p j) t -> p j t", j=4)
            nc.sync.dma_start(out=x_raw[a][:, 0:2, :], in_=rows[:, 0:2, :])
            for t0 in (0, HALF):
                nc.sync.dma_start(out=x_raw[a][:, 2:4, t0 : t0 + HALF], in_=rows[:, 2:4, t0 : t0 + HALF])
            if a == 0:
                nc.sync.dma_start(offs_t[:], offs)

        w_rows = w_words.rearrange("e a p c -> p (e a) c")
        ws_rows = w_scales.rearrange("e a q n -> q (e a) n")
        nc.sync.dma_start(out=w_t[:].bitcast(I32), in_=w_rows.bitcast(I32))
        nc.sync.dma_start(out=b_t[:], in_=b)
        for r, pos in enumerate((pos1, pos2, pos3, pos4)):
            nc.sync.dma_start(pos_t[r][:], pos)

        nc.vector.memset(warm[:, 0:1], 0.0)
        nc.scalar.activation(warm[:, 1:2], warm[:, 0:1], ACT.Relu)
        nc.vector.memset(planes[:].bitcast(I32), 0)
        nc.vector.memset(all_codes[:, A * T :], 0)

        def interleave(copy, a, t0, t1):
            run = 4 if t0 < HALF else 2
            copy(
                x_bf[a][:, t0:t1, :].rearrange("p (c i) j -> p c j i", i=run),
                x_raw[a][:, :, t0:t1].rearrange("p j (c i) -> p c j i", i=run),
            )

        def quantise(a, t0, t1):
            nc.vector.quantize_mx(
                out=codes[a][:, t0:t1].bitcast(FP8X4),
                scales=planes[4 * a : P, t0:t1],
                in_=x_bf[a][:, t0:t1, :].rearrange("p t j -> p (t j)"),
            )

        def gather_words(a, s0, s1, tag=None, words=None):
            if words is None:
                words = keep.tile(
                    [P, s1 - s0], I32, name=f"slot_codes{a}_{s0}", tag=tag or f"slot_codes{a}_{s0}", align_bytes=64
                )[:]
            for s in range(s0, s1, N):
                slot_codes[(a, s)] = words[:, s - s0 : s - s0 + N]
            width = max(704, -(-(s1 - s0) * 4 // 3 // 32) * 32) if s1 - s0 <= 1536 else 2 * (s1 - s0)
            nc.vector.tensor_copy(
                words.bitcast(U32),
                codes[a][:, 0:width].bitcast(U32).indirect(offs_t[:, s0 // 16 : s1 // 16]),
            )

        def gather_bytes(s0, s1):
            nc.vector.tensor_copy(slot_planes[0][:, s0:s1], planes[:].indirect(offs_t[:, s0 // 16 : s1 // 16]))
            for a in (1, 2):
                for q in range(4):
                    nc.sync.dma_start(
                        out=slot_planes[a][32 * q : 32 * q + 4, s0:s1].bitcast(I32),
                        in_=slot_planes[0][32 * q + 4 * a : 32 * q + 4 * a + 4, s0:s1].bitcast(I32),
                    )

        acc = {}

        def multiply(e, h, a, opens, closes):
            cols = slice(e * C + h * N, e * C + h * N + N)
            nc.tensor.matmul_mx(
                out=acc[(e, h)],
                lhsT=w_t[:, e * A + a, :].bitcast(FP4X4),
                lhsT_scale=ws_t[:, e * A + a, :],
                rhs=slot_codes[(a, e * C + h * N)].bitcast(FP8X4),
                rhs_scale=slot_planes[a][:, cols],
                start=opens,
                stop=closes,
            )

        groups = [((0, 0), (0, 1), (1, 0), (1, 1))]
        groups.extend(((e, 0), (e, 1)) for e in range(2, 7))
        groups.extend(((7, h),) for h in range(2))

        def multiply_group(g, a, last=False):
            for i, (e, h) in enumerate(groups[g]):
                multiply(e, h, a, opens=(a == 0 and i == 0), closes=(last and i == len(groups[g]) - 1))

        def open_bank(g):
            bank = psum.tile([P, 512], F32, name=f"acc{g}", tag=f"bank{g}")
            for i, (e, h) in enumerate(groups[g]):
                acc[(e, h)] = bank[:, i * N : (i + 1) * N]
                if h == 0:
                    acc[e] = bank[:, i * N : (i + 2) * N]

        interleave(nc.vector.tensor_copy, 0, 0, 160)
        interleave(nc.scalar.copy, 0, 160, 256)
        quantise(0, 0, 256)
        interleave(nc.vector.tensor_copy, 0, 256, 384)
        interleave(nc.scalar.copy, 0, 384, 512)
        quantise(0, 256, 384)
        quantise(0, 384, 512)
        ws_t = reuse.tile([P, E * A, N], U8, name="ws_t", align_bytes=64, offset=0)
        nc.gpsimd.memset(ws_t[:].rearrange("p i n -> p (i n)").bitcast(I32), 0)
        for q in range(4):
            nc.sync.dma_start(
                out=ws_t[32 * q : 32 * q + 4, :, :].bitcast(I32),
                in_=ws_rows[4 * q : 4 * q + 4, :, :].bitcast(I32),
            )
        moved_planes = reuse.tile([P, 2 * SLOTS], U8, name="moved_planes", align_bytes=64, offset=E * A * N)
        nc.gpsimd.memset(moved_planes[:].bitcast(I32), 0)
        slot_planes = [gathered_planes[:], moved_planes[:, 0:SLOTS], moved_planes[:, SLOTS : 2 * SLOTS]]
        gather_words(0, 0, 1792)
        for t0 in (0, HALF):
            interleave(nc.scalar.copy, 1, t0, t0 + HALF)
        quantise(1, 0, 512)
        ident = keep.tile([P, P], F32, name="ident", tag="share1", align_bytes=64)
        make_identity(nc, ident[:])
        gather_words(0, 1792, 2048, tag="raw1")
        for t0 in (0, HALF):
            interleave(nc.scalar.copy, 2, t0, t0 + HALF)
        gather_words(1, 0, 512)
        quantise(2, 0, 512)
        gather_words(1, 512, 640, tag="raw2")
        gather_bytes(0, 1024)
        gather_bytes(1024, 2048)
        gates = keep.tile([P, TOP * 3 * P + 16], F32, name="gates", tag="planes", align_bytes=64)
        gate_rows = gates[:, 0 : TOP * 3 * P].rearrange("p (r t) -> p r t", r=TOP)
        gate_cols = gates[:, TOP * 3 * P :].rearrange("p (b r) -> p b r", b=2)
        nc.sync.dma_start(out=gate_rows[:, 0:2, :], in_=gate[0:2, :, 0 : 3 * P].rearrange("r p t -> p r t"))
        nc.sync.dma_start(
            out=gate_rows[:, 2:TOP, 0 : 2 * P], in_=gate[2:TOP, :, 0 : 2 * P].rearrange("r p t -> p r t")
        )
        with nc.allow_non_contiguous_dma(reason="one gate value a partition"):
            nc.sync.dma_start(out=gate_cols[:, 1, 0:TOP], in_=gate[:, 0, 3 * P : T].rearrange("r p -> p r"))
            nc.sync.dma_start(out=gate_cols[:, 0, 2:TOP], in_=gate[2:TOP, 0, 2 * P : 3 * P].rearrange("r p -> p r"))
        for g in range(len(groups)):
            open_bank(g)
            multiply_group(g, 0)

        def finish_pair(i):
            rel_pair = keep.tile([P, 2 * C], F32, name=f"rel_pair{i}", tag="rel")
            for e in (2 * i, 2 * i + 1):
                nc.scalar.activation(
                    rel_pair[:, (e % 2) * C : (e % 2 + 1) * C], acc[e], ACT.Relu, bias=b_t[:, e : e + 1]
                )
            nc.scalar.activation(y_t[:, 512 * i : 512 * i + 512], rel_pair[:], ACT.Square)

        late_words = keep.tile([P, 1408], I32, name="late_words", tag="share2", align_bytes=64)
        multiply_group(0, 1)
        gather_words(2, 0, 1024)
        multiply_group(0, 2, last=True)
        finish_pair(0)
        for g in (1, 2):
            multiply_group(g, 2)
        gather_words(1, 640, 1536, words=late_words[:, 0:896])
        for g in (1, 2):
            multiply_group(g, 1, last=True)
        finish_pair(1)
        for g in (3, 4):
            multiply_group(g, 1)
        gather_words(2, 1024, 1536)
        for g in (3, 4):
            multiply_group(g, 2, last=True)
        finish_pair(2)
        gather_words(2, 1536, 2048)
        for g in (5, 6, 7):
            multiply_group(g, 2)
        gather_words(1, 1536, 1792, words=late_words[:, 896:1152])
        multiply_group(5, 1, last=True)
        rel6 = keep.tile([P, C], F32, name="rel6", tag="rel")
        nc.scalar.activation(rel6[:], acc[6], ACT.Relu, bias=b_t[:, 6:7])
        nc.scalar.activation(y_t[:, 6 * C : 7 * C], rel6[:], ACT.Square)
        gather_words(1, 1792, 1920, words=late_words[:, 1152:1280])
        multiply_group(6, 1, last=True)
        gather_words(1, 1920, 2048, words=late_words[:, 1280:1408])
        multiply_group(7, 1, last=True)
        rel7 = [keep.tile([P, N], F32, name=f"rel7_{h}") for h in range(2)]
        for h in range(2):
            nc.vector.tensor_scalar(rel7[h][:], acc[(7, h)], b_t[:, 7:8], 0.0, ALU.add, ALU.max)
        for h in range(2):
            nc.vector.tensor_tensor(y_t[:, 7 * C + h * N : 7 * C + (h + 1) * N], rel7[h][:], rel7[h][:], ALU.mult)

        own, mixed = 2 * P, 3 * P
        shared = 2
        plain = {}
        scalar_order = list(range(shared, TOP)) + list(range(shared))
        for r in scalar_order:
            t0 = mixed if r < shared else own
            plain[r] = keep.tile([P, T - t0], F32, name=f"plain{r}")
            nc.scalar.activation(plain[r][:], y_t[:].indirect(pos_t[r][:, t0 // 16 : T // 16]), ACT.Copy)
        products = {}

        def fetch(r):
            t1 = mixed if r < shared else own
            products[r] = keep.tile([P, t1], F32, name=f"product{r}")
            nc.vector.tensor_tensor(
                products[r][:], y_t[:].indirect(pos_t[r][:, 0 : t1 // 16]), gate_rows[:, r, 0:t1], ALU.mult
            )

        def add(name, width, left, right):
            total = keep.tile([P, width], F32, name=name)
            nc.vector.tensor_tensor(total[:], left, right, ALU.add)
            return total

        units = [(r, blk) for r in scalar_order for blk in ((3,) if r < shared else (2, 3))]
        turned = {}
        for i, (r, blk) in enumerate(units):
            bank = psum.tile([P, 512], F32, name=f"turned{r}_{blk}", tag=f"bank{i % 6}")
            turned[(r, blk)] = bank[:, 0:P]
            t0 = mixed if r < shared else own
            nc.tensor.transpose(turned[(r, blk)], plain[r][:, blk * P - t0 : (blk + 1) * P - t0], ident[:])
        partial = {}
        for blk in (2, 3):
            bank = psum.tile([P, 512], F32, name=f"partial{blk}", tag=f"bank{blk + 4}")
            partial[blk] = bank[:, 0:P]
        for r, blk in units:
            lists = [u for u, v in units if v == blk]
            gated = keep.tile([P, P], F32, name=f"gated{r}_{blk}")
            nc.scalar.activation(gated[:], turned[(r, blk)], ACT.Copy, scale=gate_cols[:, blk - 2, r : r + 1])
            nc.tensor.matmul(
                partial[blk], gated[:], ident[:], start=(r == lists[0]), stop=(r == lists[-1]), is_transpose=True
            )
        last_block = keep.tile([P, P], F32, name="last_block")
        nc.scalar.copy(last_block[:], partial[3])
        nc.sync.dma_start(out=out[:, mixed:T], in_=last_block[:])

        fetch(0)
        fetch(1)
        fetch(2)
        first = add("first", mixed, products[0][:], products[1][:])
        fetch(3)
        second = [
            add(f"second{h}", P, first[:, h * P : (h + 1) * P], products[2][:, h * P : (h + 1) * P]) for h in range(2)
        ]
        third_block = add("third_block", P, partial[2], first[:, own:mixed])
        nc.sync.dma_start(out=out[:, own:mixed], in_=third_block[:])
        for h in range(2):
            result = add(f"result{h}", P, second[h][:], products[3][:, h * P : (h + 1) * P])
            nc.sync.dma_start(out=out[:, h * P : (h + 1) * P], in_=result[:])
